import numpy as np
import ml_dtypes


def mxq(x, axis, fmt="e4m3"):
    dtype, down = {"e4m3": (ml_dtypes.float8_e4m3fn, 7), "e5m2": (ml_dtypes.float8_e5m2, 14)}[fmt]
    v = np.moveaxis(np.asarray(x, np.float32).astype(ml_dtypes.bfloat16).astype(np.float64), axis, -1)
    blocks = v.reshape(v.shape[:-1] + (-1, 32))
    amax = np.abs(blocks).max(-1, keepdims=True)
    byte = np.maximum(np.where(amax > 0, np.frexp(amax)[1] - 1 + 127, 0) - down, 1)
    scale = np.exp2(byte - 127.0)
    codes = (blocks / scale).astype(np.float32).astype(dtype).astype(np.float64)
    return np.moveaxis((codes * scale).reshape(v.shape), -1, axis)


WIDE = False


def mx_kscale(k):
    if not WIDE:
        return np.ones(k)
    levels = np.array([10, -10, 5, -5, 0])
    if k % 512:
        return np.exp2(np.random.permutation(np.resize(levels, k // 32))).repeat(32)
    a = np.empty((k // 512, 16))
    for p in range(k // 512):
        a[p, :8] = np.random.permutation(np.resize(levels, 8))
        for g in range(8):
            far = levels[np.abs(levels - a[p, g]) >= 10]
            a[p, g + 8] = far[np.random.randint(len(far))]
    return np.exp2(a.ravel()).repeat(32)


BF16 = ml_dtypes.bfloat16


def bf(x):
    return np.asarray(x, np.float32).astype(BF16)


def f64(x):
    return np.asarray(x).astype(np.float64)


E2M1 = np.array([0.0, 0.5, 1.0, 1.5, 2.0, 3.0, 4.0, 6.0, -0.0, -0.5, -1.0, -1.5, -2.0, -3.0, -4.0, -6.0])


def pack_weight(w, fmt):
    k, n = w.shape
    w = f64(bf(w)).reshape(k // 32, 32, n)
    amax = np.abs(w).max(1)
    if fmt == "e4m3":
        byte = np.frexp(amax)[1] - 1 + 127 - 7
    else:
        mant, ex = np.frexp(amax / 6.0)
        byte = np.where(mant > 0.5, ex, ex - 1) + 127
    byte = np.clip(np.where(amax > 0, byte, 1), 1, 254)
    scaled = (w * np.exp2(127.0 - byte)[:, None, :]).reshape(k, n).astype(np.float32)
    by_word = np.ascontiguousarray(scaled.reshape(k // 512, 128, 4, n).transpose(0, 1, 3, 2))
    if fmt == "e4m3":
        words = by_word.astype(ml_dtypes.float8_e4m3fn).view(np.uint8)
    else:
        c = by_word.astype(ml_dtypes.float4_e2m1fn).view(np.uint8) & 0xF
        words = c[..., 0::2] | (c[..., 1::2] << 4)
    return np.ascontiguousarray(words), np.ascontiguousarray(byte.astype(np.uint8).reshape(k // 512, 16, n))


def unpack_weight(words, scales, fmt):
    g, p, n, _ = words.shape
    if fmt == "e4m3":
        vals = np.ascontiguousarray(words).view(ml_dtypes.float8_e4m3fn).astype(np.float64)
    else:
        nib = np.empty((g, p, n, 4), np.uint8)
        nib[..., 0::2] = words & 0xF
        nib[..., 1::2] = words >> 4
        vals = E2M1[nib]
    vals = vals * np.repeat(np.exp2(scales.astype(np.float64) - 127.0), 8, axis=1)[..., None]
    return vals.transpose(0, 1, 3, 2).reshape(g * 512, n)
def pack4(w):
    words, scales = pack_weight(w, "e2m1")
    return words.reshape(words.shape[0], 128, -1), scales


def unpack4(words, scales):
    return unpack_weight(words.reshape(words.shape[0], 128, -1, 2), scales, "e2m1")


def planes(Y):
    n, m = Y.shape
    b = f64(bf(Y)).reshape(n // 32, 32, m)
    amax = np.abs(b).max(1)
    byte = np.clip(np.where(amax > 0, np.frexp(amax)[1] - 1 + 127 - 7, 1), 1, 254)
    codes = (b * np.exp2(127.0 - byte)[:, None, :]).reshape(n, m).astype(np.float32).astype(ml_dtypes.float8_e4m3fn).view(np.uint8)
    words = codes.reshape(n // 512, 128, 4, m).transpose(0, 1, 3, 2)
    return np.ascontiguousarray(words), np.ascontiguousarray(byte.astype(np.uint8).reshape(n // 512, 16, m))


S, R, H, E = 2, 512, 4, 128
D = H * E
EPS = 1e-5


def gain_layer_norm(x, gain):
    mean = np.mean(x, axis=-1, keepdims=True)
    var = np.mean(np.square(x - mean), axis=-1, keepdims=True)
    return (x - mean) / np.sqrt(var + EPS) * gain


def sigmoid(v):
    return 1.0 / (1.0 + np.exp(-v))


def softmax(v):
    e = np.exp(v - v.max(-1, keepdims=True))
    return e / e.sum(-1, keepdims=True)


def setup_inputs():
    f = mx_kscale(D)
    q = mx_kscale(R)
    size = np.exp2(-8.0 * np.random.random_sample((S, R, 1)))
    m = bf((0.5 + 1.5 * np.random.standard_normal((S, R, D))) * size)
    ln_g = bf((1.0 + 0.1 * np.random.standard_normal(D)) * f)
    w_v_words, w_v_scales = pack4(np.random.standard_normal((D, D)) / np.sqrt(D) / f[:, None])
    w_g_words, w_g_scales = pack4(np.random.standard_normal((D, D)) / np.sqrt(D) / f[:, None])
    return {
        "m": m,
        "ln_g": ln_g,
        "w_v_words": w_v_words,
        "w_v_scales": w_v_scales,
        "w_g_words": w_g_words,
        "w_g_scales": w_g_scales,
        "t": bf((0.5 + np.random.random_sample((S, R))) / q[None, :]),
        "z": bf(np.random.standard_normal((H, R, R)) * 1.5),
        "c": bf(np.random.standard_normal((H, R)) * 0.265 * np.sqrt(R) * q[None, :]),
    }


def core(m, ln_g, w_v_words, w_v_scales, w_g_words, w_g_scales, t, z, c):
    mn = gain_layer_norm(f64(m), f64(ln_g))
    mnq = mxq(mn, 2, "e4m3")
    g = sigmoid(mnq @ unpack4(w_g_words, w_g_scales)).reshape(S, R, H, E)
    v0 = (mnq @ unpack4(w_v_words, w_v_scales)).reshape(S, R, H, E)
    v = v0 * f64(t)[:, :, None, None]
    p = softmax(f64(z))
    a = p * f64(c)[:, None, :]
    vh = v.transpose(2, 1, 0, 3).reshape(H, R, S * E)
    uh = mxq(a, 2, "e4m3") @ mxq(vh, 1, "e4m3")
    u = uh.reshape(H, R, S, E).transpose(2, 1, 0, 3)
    return (g * u).reshape(S, R, D)


def reference(m, ln_g, w_v_words, w_v_scales, w_g_words, w_g_scales, t, z, c):
    R_out = core(m, ln_g, w_v_words, w_v_scales, w_g_words, w_g_scales, t, z, c)
    words, scales = planes(np.moveaxis(R_out, 2, 0).reshape(512, -1))
    return R_out, words, scales

@@ -1,0 +1,270 @@
+from contextlib import ExitStack
+
+import concourse.mybir as mybir
+from concourse.masks import make_identity
+
+S, R, H, E = 2, 512, 4, 128
+D = H * E
+P = 128
+EPS = 1e-5
+FLOPS = 2 * (2 * S * R * D * D) + 2 * H * R * R * S * E
+
+F32 = mybir.dt.float32
+BF16 = mybir.dt.bfloat16
+U32 = mybir.dt.uint32
+I32 = mybir.dt.int32
+U8 = mybir.dt.uint8
+E4M3X4 = mybir.dt.float8_e4m3fn_x4
+E2M1X4 = mybir.dt.float4_e2m1fn_x4
+ACT = mybir.ActivationFunctionType
+ALU = mybir.AluOpType
+
+
+def tile_msapairweightedaveraging_x2_kernel(tc, m, ln_g, w_v_words, w_v_scales, w_g_words, w_g_scales, t, z, c, out_0, out_1, out_2):
+    nc = tc.nc
+    with ExitStack() as ctx:
+        keep = ctx.enter_context(tc.tile_pool(name="keep", bufs=1))
+        work = ctx.enter_context(tc.tile_pool(name="work", bufs=2))
+        psum = ctx.enter_context(tc.psum_pool(name="psum", bufs=4))
+
+        m_sb = [keep.tile([P, 4, D], BF16, name=f"m{s}", align_bytes=64) for s in range(S)]
+        z_sb = [keep.tile([P, H, R], BF16, name=f"z{b}", align_bytes=64) for b in range(4)]
+        gain = keep.tile([P, 4], BF16, name="gain")
+        tmask = keep.tile([P, S, 4], BF16, name="tmask")
+        crow = keep.tile([P, R], BF16, name="crow", align_bytes=64)
+        words = [keep.tile([P, 2 * D], U8, name=f"words{i}", align_bytes=64) for i in range(2)]
+        wsc = [keep.tile([P, D], U8, name=f"wsc{i}", align_bytes=64) for i in range(2)]
+
+        nc.vector.memset(crow[:], 0.0)
+        for i in range(2):
+            nc.vector.memset(wsc[i][:].bitcast(I32), 0)
+
+        nc.scalar.dma_start(out=crow[0:H, :], in_=c)
+        nc.scalar.dma_start(out=gain[:], in_=ln_g.rearrange("(p t) -> p t", t=4))
+        nc.scalar.dma_start(out=tmask[:], in_=t.rearrange("s (p t) -> p s t", t=4))
+
+        def load_m(s):
+            src = m[s].rearrange("(p t) d -> p t d", t=4)
+            for half in range(2):
+                nc.sync.dma_start(out=m_sb[s][:, 2 * half : 2 * half + 2, :], in_=src[:, 2 * half : 2 * half + 2, :])
+
+        def load_z(b):
+            src = z.rearrange("h (p b) j -> b p h j", b=4)
+            for half in range(2):
+                hs = slice(2 * half, 2 * half + 2)
+                nc.sync.dma_start(out=z_sb[b][:, hs, :], in_=src[b][:, hs, :])
+
+        load_m(0)
+        load_z(0)
+        load_z(1)
+        load_m(1)
+        for i, w in enumerate((w_v_words, w_g_words)):
+            nc.sync.dma_start(out=words[i][:].bitcast(I32), in_=w[0].bitcast(I32))
+        for i, ws in enumerate((w_v_scales, w_g_scales)):
+            for q in range(4):
+                nc.sync.dma_start(out=wsc[i][32 * q : 32 * q + 4, :].bitcast(I32), in_=ws[0, 4 * q : 4 * q + 4, :].bitcast(I32))
+        load_z(2)
+        load_z(3)
+
+        ident = keep.tile([P, P], F32, name="ident", align_bytes=64)
+        make_identity(nc, ident[:])
+        ident_bf = keep.tile([P, P], BF16, name="ident_bf", align_bytes=64)
+        nc.vector.tensor_copy(out=ident_bf[:], in_=ident[:])
+        half_pow = keep.tile([P, 4], F32, name="half_pow")
+        nc.gpsimd.memset(half_pow[:], -0.5)
+        tmask_f = keep.tile([P, S, 4], F32, name="tmask_f")
+        nc.vector.tensor_copy(out=tmask_f[:], in_=tmask[:])
+
+        c_half = keep.tile([P, H, R], BF16, name="c_half", align_bytes=64)
+        for h in range(H):
+            cps = psum.tile([P, R], F32, name="mm", bufs=4)
+            nc.tensor.matmul(out=cps[:], lhsT=ident_bf[:, h : h + 1].to_broadcast([P, P]), rhs=crow[:], start=True, stop=True)
+            nc.scalar.mul(out=c_half[:, h, :], in_=cps[:], mul=0.5)
+
+        mv = [keep.tile([P, 4, 2], F32, name=f"mv{s}") for s in range(S)]
+        ve = [keep.tile([P, 4], F32, name=f"ve{s}") for s in range(S)]
+        rstd = [keep.tile([P, 4], F32, name=f"rstd{s}") for s in range(S)]
+        negmean = [keep.tile([P, 4], F32, name=f"negmean{s}") for s in range(S)]
+        mnb = [keep.tile([P, R, 4], BF16, name=f"mnb{s}", align_bytes=64) for s in range(S)]
+        mnq = [keep.tile([P, R], U32, name=f"mnq{s}", align_bytes=64) for s in range(S)]
+        mns = [keep.tile([P, R], U8, name=f"mns{s}", align_bytes=64) for s in range(S)]
+        vtmp = [keep.tile([P, 4, D], BF16, name=f"vtmp{s}", align_bytes=64) for s in range(S)]
+        vin = [keep.tile([P, D, 4], BF16, name=f"vin{s}", align_bytes=64) for s in range(S)]
+        vq = [keep.tile([P, D], U32, name=f"vq{s}", align_bytes=64) for s in range(S)]
+        vs = [keep.tile([P, D], U8, name=f"vs{s}", align_bytes=64) for s in range(S)]
+        negmax = [keep.tile([P, H], F32, name=f"negmax{b}") for b in range(4)]
+        sums = [keep.tile([P, H], F32, name=f"sums{b}") for b in range(4)]
+        rinv = [keep.tile([P, H], F32, name=f"rinv{b}") for b in range(4)]
+        e_sb = [[None] * H for b in range(4)]
+        a_bf = [None] * 4
+        aq = [keep.tile([P, H * P], U32, name=f"aq{b}", align_bytes=64) for b in range(4)]
+        asc = [keep.tile([P, H * P], U8, name=f"asc{b}", align_bytes=64) for b in range(4)]
+        ain = [None] * 4
+        th = [[None] * 4 for s in range(S)]
+        ob = [[None] * 2 for s in range(S)]
+        oin = [keep.tile([P, R, 4], BF16, name=f"oin{s}", align_bytes=64) for s in range(S)]
+        oq = [keep.tile([P, R], U32, name=f"oq{s}", align_bytes=64) for s in range(S)]
+        osc = [keep.tile([P, R], U8, name=f"osc{s}", align_bytes=64) for s in range(S)]
+
+        def stats(s):
+            st = work.tile([P, 4, 6], F32, name="bnst")
+            for j in range(4):
+                nc.vector.bn_stats(out=st[:, j, :], in_=m_sb[s][:, j, :])
+            for j in range(4):
+                nc.vector.bn_aggr(out=mv[s][:, j, :], in_=st[:, j, :])
+            nc.gpsimd.tensor_scalar(out=ve[s][:], in0=mv[s][:, :, 1], scalar1=EPS, scalar2=1.0, op0=ALU.add, op1=ALU.mult)
+            nc.gpsimd.tensor_tensor(out=rstd[s][:], in0=ve[s][:], in1=half_pow[:], op=ALU.pow)
+            nc.gpsimd.tensor_scalar(out=negmean[s][:], in0=mv[s][:, :, 0], scalar1=-1.0, scalar2=0.0, op0=ALU.mult, op1=ALU.add)
+
+        def norm(s, j):
+            xn = work.tile([P, 4, P], F32, name="xn", bufs=4, align_bytes=64)
+            nc.gpsimd.tensor_scalar(out=xn[:], in0=m_sb[s][:, j, :].rearrange("q (p t) -> q t p", t=4),
+                                    scalar1=negmean[s][:, j : j + 1], scalar2=rstd[s][:, j : j + 1], op0=ALU.add, op1=ALU.mult)
+            tr = psum.tile([P, 4, P], F32, name="tr", bufs=4)
+            for u in range(4):
+                nc.tensor.transpose(tr[:, u, :], xn[:, u, :], ident[:])
+            nc.vector.tensor_tensor(out=mnb[s][:, j * P : (j + 1) * P, :], in0=tr[:].rearrange("p t q -> p q t"),
+                                    in1=gain[:].unsqueeze(1).to_broadcast([P, P, 4]), op=ALU.mult)
+
+        def qmn(s):
+            nc.vector.quantize_mx(out=mnq[s][:].bitcast(E4M3X4), scales=mns[s][:], in_=mnb[s][:].rearrange("p c t -> p (c t)"))
+
+        def first_stage(s, j, i):
+            ps = psum.tile([P, D], F32, name="mm", bufs=4)
+            cols = slice(j * P, (j + 1) * P)
+            nc.tensor.matmul_mx(out=ps[:], lhsT=mnq[s][:, cols].bitcast(E4M3X4), lhsT_scale=mns[s][:, cols],
+                                rhs=words[i][:].bitcast(E2M1X4), rhs_scale=wsc[i][:], start=True, stop=True)
+            return ps
+
+        def values(s):
+            for j in range(4):
+                ps = first_stage(s, j, 0)
+                nc.scalar.activation(out=vtmp[s][:, j, :], in_=ps[:], func=ACT.Copy, scale=tmask_f[:, s, j : j + 1])
+            nc.gpsimd.tensor_scalar(out=vin[s][:], in0=vtmp[s][:].rearrange("p t f -> p f t"), scalar1=1.0, scalar2=0.0, op0=ALU.mult, op1=ALU.add)
+
+        def qv(s):
+            nc.vector.quantize_mx(out=vq[s][:].bitcast(E4M3X4), scales=vs[s][:], in_=vin[s][:].rearrange("p c t -> p (c t)"))
+
+        def gate(s, b):
+            ps = first_stage(s, b, 1)
+            g = work.tile([P, D], F32, name="th", bufs=4, align_bytes=64)
+            th[s][b] = g
+            nc.scalar.activation(out=g[:], in_=ps[:], func=ACT.Tanh, scale=0.5)
+
+        def rowmax(b, h):
+            junk = work.tile([P, R], BF16, name="junk", bufs=2)
+            nc.vector.tensor_scalar(out=junk[:], in0=z_sb[b][:, h, :], scalar1=-1.0, scalar2=None, op0=ALU.mult, op1=ALU.min, accum_out=negmax[b][:, h : h + 1])
+
+        def expo(b, h):
+            e = work.tile([P, R], F32, name="e", bufs=8, align_bytes=64)
+            e_sb[b][h] = e
+            nc.scalar.activation(out=e[:], in_=z_sb[b][:, h, :], func=ACT.Exp, bias=negmax[b][:, h : h + 1], scale=1.0, accum_out=sums[b][:, h : h + 1])
+
+        def weights(b):
+            nc.vector.reciprocal(out=rinv[b][:], in_=sums[b][:])
+            a = work.tile([P, H, R], BF16, name="a_bf", bufs=2, align_bytes=64)
+            a_bf[b] = a
+            for h in range(H):
+                nc.vector.scalar_tensor_tensor(out=a[:, h, :], in0=e_sb[b][h][:], scalar=rinv[b][:, h : h + 1], in1=c_half[:, h, :], op0=ALU.mult, op1=ALU.mult)
+
+        def turn_weights(b):
+            ai = work.tile([P, H * P, 4], BF16, name="ain", bufs=2, align_bytes=64)
+            ain[b] = ai
+            for hh in range(2):
+                tr = psum.tile([P, 2, 2, P], F32, name="tr", bufs=4)
+                for k in range(2):
+                    aw = a_bf[b][:, 2 * hh + k, :].bitcast(F32)
+                    for u in range(2):
+                        nc.tensor.transpose(tr[:, k, u, :], aw[:, u::2], ident[:])
+                dst = ai[:, 2 * hh * P : 2 * (hh + 1) * P, :].rearrange("p c t -> p (c t)").bitcast(F32).rearrange("p (k q u) -> p k q u", k=2, u=2)
+                nc.scalar.copy(out=dst, in_=tr[:].rearrange("p k u q -> p k q u"))
+
+        def qa(b):
+            nc.vector.quantize_mx(out=aq[b][:].bitcast(E4M3X4), scales=asc[b][:], in_=ain[b][:].rearrange("p c t -> p (c t)"))
+
+        def product(s, b):
+            ps = psum.tile([P, D], F32, name="mm", bufs=4)
+            for h in range(H):
+                cols = slice(h * P, (h + 1) * P)
+                nc.tensor.matmul_mx(out=ps[:, cols], lhsT=aq[b][:, cols].bitcast(E4M3X4), lhsT_scale=asc[b][:, cols],
+                                    rhs=vq[s][:, cols].bitcast(E4M3X4), rhs_scale=vs[s][:, cols], start=True, stop=True)
+            o = work.tile([P, D], F32, name="o", bufs=4, align_bytes=64)
+            nc.vector.scalar_tensor_tensor(out=o[:], in0=th[s][b][:], scalar=1.0, in1=ps[:], op0=ALU.add, op1=ALU.mult)
+            nc.sync.dma_start(out=out_0[s].rearrange("(p b) d -> b p d", b=4)[b], in_=o[:])
+            if b % 2 == 0:
+                obt = work.tile([P, 2, D], BF16, name="ob", bufs=4, align_bytes=64)
+                ob[s][b // 2] = obt
+            nc.scalar.copy(out=ob[s][b // 2][:, b % 2, :], in_=o[:])
+
+        def turn_out(s, w):
+            tr = psum.tile([P, 2, 2, P], F32, name="tr", bufs=4)
+            for k in range(2):
+                ow = ob[s][w][:, k, :].bitcast(F32)
+                for u in range(2):
+                    nc.tensor.transpose(tr[:, k, u, :], ow[:, u::2], ident[:])
+            dst = oin[s][:].rearrange("p c t -> p (c t)").bitcast(F32).rearrange("p (q x) -> p q x", x=8)
+            nc.scalar.copy(out=dst[:, :, 4 * w : 4 * w + 4], in_=tr[:].rearrange("p k u q -> p q (k u)"))
+
+        def planes(s):
+            nc.vector.quantize_mx(out=oq[s][:].bitcast(E4M3X4), scales=osc[s][:], in_=oin[s][:].rearrange("p c t -> p (c t)"))
+            cols = slice(s * R, (s + 1) * R)
+            nc.sync.dma_start(out=out_1[0, :, cols, :].rearrange("p m t -> p (m t)").bitcast(I32), in_=oq[s][:].bitcast(I32))
+            for q in range(4):
+                nc.sync.dma_start(out=out_2[0, 4 * q : 4 * q + 4, cols].bitcast(I32), in_=osc[s][32 * q : 32 * q + 4, :].bitcast(I32))
+
+        def softmax_head(b):
+            for h in range(H):
+                rowmax(b, h)
+                expo(b, h)
+
+        stats(0)
+        softmax_head(0)
+        for j in range(4):
+            norm(0, j)
+            rowmax(1, j)
+            expo(1, j)
+        qmn(0)
+        values(0)
+        stats(1)
+        weights(0)
+        turn_weights(0)
+        for j in range(4):
+            norm(1, j)
+        qa(0)
+        qmn(1)
+        values(1)
+        softmax_head(2)
+        qv(0)
+        weights(1)
+        turn_weights(1)
+        gate(0, 0)
+        gate(1, 0)
+        qv(1)
+        qa(1)
+        product(0, 0)
+        product(1, 0)
+        softmax_head(3)
+        weights(2)
+        turn_weights(2)
+        gate(0, 1)
+        gate(1, 1)
+        product(0, 1)
+        product(1, 1)
+        turn_out(0, 0)
+        turn_out(1, 0)
+        qa(2)
+        weights(3)
+        turn_weights(3)
+        gate(0, 2)
+        gate(1, 2)
+        product(0, 2)
+        product(1, 2)
+        qa(3)
+        gate(0, 3)
+        gate(1, 3)
+        product(0, 3)
+        turn_out(0, 1)
+        product(1, 3)
+        turn_out(1, 1)
+        planes(0)
+        planes(1)

@@ -26,65 +26,66 @@ def tile_msapairweightedaveraging_x2_kernel(tc, m, ln_g, w_v_words, w_v_scales, 
         keep = ctx.enter_context(tc.tile_pool(name="keep", bufs=1))
         work = ctx.enter_context(tc.tile_pool(name="work", bufs=2))
         psum = ctx.enter_context(tc.psum_pool(name="psum", bufs=4))
-
+        ctx.enter_context(tc.manual_schedule())
         m_sb = [keep.tile([P, 4, D], BF16, name=f"m{s}", align_bytes=64) for s in range(S)]
-        z_sb = [keep.tile([P, H, R], BF16, name=f"z{b}", align_bytes=64) for b in range(4)]
+        z_sb = [keep.tile([P, H, 2, R], BF16, name=f"z{w}", align_bytes=64) for w in range(2)]
         gain = keep.tile([P, 4], BF16, name="gain")
         tmask = keep.tile([P, S, 4], BF16, name="tmask")
-        crow = keep.tile([P, R], BF16, name="crow", align_bytes=64)
         words = [keep.tile([P, 2 * D], U8, name=f"words{i}", align_bytes=64) for i in range(2)]
         wsc = [keep.tile([P, D], U8, name=f"wsc{i}", align_bytes=64) for i in range(2)]
-
-        nc.vector.memset(crow[:], 0.0)
-        for i in range(2):
-            nc.vector.memset(wsc[i][:].bitcast(I32), 0)
-
-        nc.scalar.dma_start(out=crow[0:H, :], in_=c)
-        nc.scalar.dma_start(out=gain[:], in_=ln_g.rearrange("(p t) -> p t", t=4))
-        nc.scalar.dma_start(out=tmask[:], in_=t.rearrange("s (p t) -> p s t", t=4))
+        ident = keep.tile([P, P], F32, name="ident", align_bytes=64)
+        half_pow = keep.tile([P, 4], F32, name="half_pow")
+        tmask_f = keep.tile([P, S, 4], F32, name="tmask_f")
+        c_all = keep.tile([P, H, R], BF16, name="c_all", align_bytes=64)
 
         def load_m(s):
             src = m[s].rearrange("(p t) d -> p t d", t=4)
             for half in range(2):
                 nc.sync.dma_start(out=m_sb[s][:, 2 * half : 2 * half + 2, :], in_=src[:, 2 * half : 2 * half + 2, :])
 
-        def load_z(b):
-            src = z.rearrange("h (p b) j -> b p h j", b=4)
+        def load_z(w):
+            src = z.rearrange("h (p w b) j -> w p h b j", w=2, b=2)
             for half in range(2):
                 hs = slice(2 * half, 2 * half + 2)
-                nc.sync.dma_start(out=z_sb[b][:, hs, :], in_=src[b][:, hs, :])
+                nc.sync.dma_start(out=z_sb[w][:, hs, :, :], in_=src[w][:, hs, :, :])
 
-        load_m(0)
-        load_z(0)
-        load_z(1)
-        load_m(1)
-        for i, w in enumerate((w_v_words, w_g_words)):
-            nc.sync.dma_start(out=words[i][:].bitcast(I32), in_=w[0].bitcast(I32))
-        for i, ws in enumerate((w_v_scales, w_g_scales)):
-            for q in range(4):
-                nc.sync.dma_start(out=wsc[i][32 * q : 32 * q + 4, :].bitcast(I32), in_=ws[0, 4 * q : 4 * q + 4, :].bitcast(I32))
-        load_z(2)
-        load_z(3)
+        def load_words():
+            for i, w in enumerate((w_v_words, w_g_words)):
+                nc.sync.dma_start(out=words[i][:].bitcast(I32), in_=w[0].bitcast(I32))
 
-        ident = keep.tile([P, P], F32, name="ident", align_bytes=64)
-        make_identity(nc, ident[:])
-        ident_bf = keep.tile([P, P], BF16, name="ident_bf", align_bytes=64)
-        nc.vector.tensor_copy(out=ident_bf[:], in_=ident[:])
-        half_pow = keep.tile([P, 4], F32, name="half_pow")
-        nc.gpsimd.memset(half_pow[:], -0.5)
-        tmask_f = keep.tile([P, S, 4], F32, name="tmask_f")
-        nc.vector.tensor_copy(out=tmask_f[:], in_=tmask[:])
+        def load_small():
+            for i in range(2):
+                nc.vector.memset(wsc[i][:].bitcast(I32), 0)
+            warm = keep.tile([P, 1], F32, name="warm")
+            nc.vector.memset(warm[:], 0.0)
+            nc.scalar.activation(out=warm[:], in_=warm[:], func=ACT.Exp)
 
-        c_half = keep.tile([P, H, R], BF16, name="c_half", align_bytes=64)
-        for h in range(H):
-            cps = psum.tile([P, R], F32, name="mm", bufs=4)
-            nc.tensor.matmul(out=cps[:], lhsT=ident_bf[:, h : h + 1].to_broadcast([P, P]), rhs=crow[:], start=True, stop=True)
-            nc.scalar.mul(out=c_half[:, h, :], in_=cps[:], mul=0.5)
+        def load_vectors():
+            nc.sync.dma_start(out=gain[:], in_=ln_g.rearrange("(p t) -> p t", t=4))
+            nc.sync.dma_start(out=tmask[:], in_=t.rearrange("s (p t) -> p s t", t=4))
 
+        def load_scales():
+            for i, ws in enumerate((w_v_scales, w_g_scales)):
+                for q in range(4):
+                    nc.sync.dma_start(out=wsc[i][32 * q : 32 * q + 4, :].bitcast(I32), in_=ws[0, 4 * q : 4 * q + 4, :].bitcast(I32))
+
+        def constants():
+            make_identity(nc, ident[:])
+            nc.gpsimd.memset(half_pow[:], -0.5)
+            nc.gpsimd.tensor_scalar(out=tmask_f[:], in0=tmask[:], scalar1=0.5, scalar2=0.0, op0=ALU.mult, op1=ALU.add)
+
+        def load_c():
+            nc.sync.dma_start(out=c_all[:].rearrange("p h j -> p (h j)"), in_=c.rearrange("h j -> (h j)").partition_broadcast(P))
+
+        st = [keep.tile([P, 4, 6], F32, name=f"st{s}") for s in range(S)]
         mv = [keep.tile([P, 4, 2], F32, name=f"mv{s}") for s in range(S)]
+        ssum = [keep.tile([P, 4], F32, name=f"ssum{s}") for s in range(S)]
+        smean = [keep.tile([P, 4], F32, name=f"smean{s}") for s in range(S)]
+        ssq = [keep.tile([P, 4], F32, name=f"ssq{s}") for s in range(S)]
         ve = [keep.tile([P, 4], F32, name=f"ve{s}") for s in range(S)]
         rstd = [keep.tile([P, 4], F32, name=f"rstd{s}") for s in range(S)]
         negmean = [keep.tile([P, 4], F32, name=f"negmean{s}") for s in range(S)]
+        nmr = [keep.tile([P, 4], F32, name=f"nmr{s}") for s in range(S)]
         mnb = [keep.tile([P, R, 4], BF16, name=f"mnb{s}", align_bytes=64) for s in range(S)]
         mnq = [keep.tile([P, R], U32, name=f"mnq{s}", align_bytes=64) for s in range(S)]
         mns = [keep.tile([P, R], U8, name=f"mns{s}", align_bytes=64) for s in range(S)]
@@ -96,175 +97,384 @@ def tile_msapairweightedaveraging_x2_kernel(tc, m, ln_g, w_v_words, w_v_scales, 
         sums = [keep.tile([P, H], F32, name=f"sums{b}") for b in range(4)]
         rinv = [keep.tile([P, H], F32, name=f"rinv{b}") for b in range(4)]
         e_sb = [[None] * H for b in range(4)]
-        a_bf = [None] * 4
+        a_bf = [keep.tile([P, H, R], BF16, name=f"a_bf{b}", align_bytes=64) for b in range(4)]
+        ain = [keep.tile([P, H * P, 4], BF16, name=f"ain{b}", align_bytes=64) for b in range(4)]
         aq = [keep.tile([P, H * P], U32, name=f"aq{b}", align_bytes=64) for b in range(4)]
         asc = [keep.tile([P, H * P], U8, name=f"asc{b}", align_bytes=64) for b in range(4)]
-        ain = [None] * 4
         th = [[None] * 4 for s in range(S)]
-        ob = [[None] * 2 for s in range(S)]
+        ob = [[keep.tile([P, 2, D], BF16, name=f"ob{s}{w}", align_bytes=64) for w in range(2)] for s in range(S)]
         oin = [keep.tile([P, R, 4], BF16, name=f"oin{s}", align_bytes=64) for s in range(S)]
         oq = [keep.tile([P, R], U32, name=f"oq{s}", align_bytes=64) for s in range(S)]
         osc = [keep.tile([P, R], U8, name=f"osc{s}", align_bytes=64) for s in range(S)]
+        o_sb = [[None] * 4 for s in range(S)]
 
-        def stats(s):
-            st = work.tile([P, 4, 6], F32, name="bnst")
-            for j in range(4):
-                nc.vector.bn_stats(out=st[:, j, :], in_=m_sb[s][:, j, :])
-            for j in range(4):
-                nc.vector.bn_aggr(out=mv[s][:, j, :], in_=st[:, j, :])
-            nc.gpsimd.tensor_scalar(out=ve[s][:], in0=mv[s][:, :, 1], scalar1=EPS, scalar2=1.0, op0=ALU.add, op1=ALU.mult)
-            nc.gpsimd.tensor_tensor(out=rstd[s][:], in0=ve[s][:], in1=half_pow[:], op=ALU.pow)
-            nc.gpsimd.tensor_scalar(out=negmean[s][:], in0=mv[s][:, :, 0], scalar1=-1.0, scalar2=0.0, op0=ALU.mult, op1=ALU.add)
+        def bn(s, j):
+            nc.vector.bn_stats(out=st[s][:, j, :], in_=m_sb[s][:, j, :])
+
+        def aggr(s, lo=0, hi=4):
+            for j in range(lo, hi):
+                nc.vector.bn_aggr(out=mv[s][:, j, :], in_=st[s][:, j, :])
+            r = slice(lo, hi)
+            nc.gpsimd.tensor_scalar(out=ve[s][:, r], in0=mv[s][:, r, 1], scalar1=EPS, scalar2=1.0, op0=ALU.add, op1=ALU.mult)
+            nc.gpsimd.tensor_tensor(out=rstd[s][:, r], in0=ve[s][:, r], in1=half_pow[:, r], op=ALU.pow)
+            nc.gpsimd.tensor_scalar(out=negmean[s][:, r], in0=mv[s][:, r, 0], scalar1=-1.0, scalar2=0.0, op0=ALU.mult, op1=ALU.add)
+
+        def sstat_sum(s, lo, hi):
+            for j in range(lo, hi):
+                sjunk = work.tile([P, D], BF16, name="sjunk", bufs=2)
+                nc.scalar.activation(out=sjunk[:], in_=m_sb[s][:, j, :], func=ACT.Copy, accum_out=ssum[s][:, j : j + 1])
+            nc.scalar.mul(out=smean[s][:, lo:hi], in_=ssum[s][:, lo:hi], mul=-1.0 / D)
+
+        def sstat_sq(s, lo, hi):
+            for j in range(lo, hi):
+                sjunk = work.tile([P, D], BF16, name="sjunk", bufs=2)
+                nc.scalar.activation(out=sjunk[:], in_=m_sb[s][:, j, :], func=ACT.Square, bias=smean[s][:, j : j + 1], accum_out=ssq[s][:, j : j + 1])
+            r = slice(lo, hi)
+            nc.gpsimd.tensor_scalar(out=negmean[s][:, r], in0=smean[s][:, r], scalar1=1.0, scalar2=0.0, op0=ALU.mult, op1=ALU.add)
+            nc.gpsimd.tensor_scalar(out=ve[s][:, r], in0=ssq[s][:, r], scalar1=1.0 / D, scalar2=EPS, op0=ALU.mult, op1=ALU.add)
+            nc.gpsimd.tensor_tensor(out=rstd[s][:, r], in0=ve[s][:, r], in1=half_pow[:, r], op=ALU.pow)
+
+
+        xn_of = {}
 
         def norm(s, j):
-            xn = work.tile([P, 4, P], F32, name="xn", bufs=4, align_bytes=64)
-            nc.gpsimd.tensor_scalar(out=xn[:], in0=m_sb[s][:, j, :].rearrange("q (p t) -> q t p", t=4),
-                                    scalar1=negmean[s][:, j : j + 1], scalar2=rstd[s][:, j : j + 1], op0=ALU.add, op1=ALU.mult)
+            xn = work.tile([P, 4, P], F32, name="xn", bufs=8, align_bytes=64)
+            xn_of[s, j] = xn
+            src = m_sb[s][:, j, :].rearrange("q (p t) -> q t p", t=4)
+            nc.gpsimd.tensor_scalar(out=xn[:], in0=src, scalar1=negmean[s][:, j : j + 1], scalar2=rstd[s][:, j : j + 1], op0=ALU.add, op1=ALU.mult)
+
+        tr_of = {}
+
+        def turn_m(s, j):
             tr = psum.tile([P, 4, P], F32, name="tr", bufs=4)
+            tr_of[s, j] = tr
             for u in range(4):
-                nc.tensor.transpose(tr[:, u, :], xn[:, u, :], ident[:])
-            nc.vector.tensor_tensor(out=mnb[s][:, j * P : (j + 1) * P, :], in0=tr[:].rearrange("p t q -> p q t"),
+                nc.tensor.transpose(tr[:, u, :], xn_of[s, j][:, u, :], ident[:])
+
+        def gainm(s, j):
+            nc.vector.tensor_tensor(out=mnb[s][:, j * P : (j + 1) * P, :], in0=tr_of[s, j][:].rearrange("p t q -> p q t"),
                                     in1=gain[:].unsqueeze(1).to_broadcast([P, P, 4]), op=ALU.mult)
 
         def qmn(s):
             nc.vector.quantize_mx(out=mnq[s][:].bitcast(E4M3X4), scales=mns[s][:], in_=mnb[s][:].rearrange("p c t -> p (c t)"))
 
-        def first_stage(s, j, i):
-            ps = psum.tile([P, D], F32, name="mm", bufs=4)
-            cols = slice(j * P, (j + 1) * P)
-            nc.tensor.matmul_mx(out=ps[:], lhsT=mnq[s][:, cols].bitcast(E4M3X4), lhsT_scale=mns[s][:, cols],
-                                rhs=words[i][:].bitcast(E2M1X4), rhs_scale=wsc[i][:], start=True, stop=True)
-            return ps
+        def mx1(out, s, j, i, cols):
+            rows = slice(j * P, (j + 1) * P)
+            nc.tensor.matmul_mx(out=out, lhsT=mnq[s][:, rows].bitcast(E4M3X4), lhsT_scale=mns[s][:, rows],
+                                rhs=words[i][:, 2 * cols.start : 2 * cols.stop].bitcast(E2M1X4), rhs_scale=wsc[i][:, cols], start=True, stop=True)
 
-        def values(s):
-            for j in range(4):
-                ps = first_stage(s, j, 0)
-                nc.scalar.activation(out=vtmp[s][:, j, :], in_=ps[:], func=ACT.Copy, scale=tmask_f[:, s, j : j + 1])
-            nc.gpsimd.tensor_scalar(out=vin[s][:], in0=vtmp[s][:].rearrange("p t f -> p f t"), scalar1=1.0, scalar2=0.0, op0=ALU.mult, op1=ALU.add)
+        vps = {}
+
+        def vals_t(s, j):
+            ps = psum.tile([P, D], F32, name="mm", bufs=4)
+            vps[s, j] = ps
+            mx1(ps[:], s, j, 0, slice(0, D))
+
+        def vals_s(s, j):
+            ps = vps[s, j]
+            nc.scalar.activation(out=vtmp[s][:, j, :], in_=ps[:], func=ACT.Copy, scale=tmask_f[:, s, j : j + 1])
+
+        def vint(s, k):
+            fs = slice(k * 256, (k + 1) * 256)
+            dst, src = vin[s][:, fs, :], vtmp[s][:, :, fs].rearrange("p t f -> p f t")
+            nc.vector.tensor_copy(out=dst, in_=src)
 
         def qv(s):
             nc.vector.quantize_mx(out=vq[s][:].bitcast(E4M3X4), scales=vs[s][:], in_=vin[s][:].rearrange("p c t -> p (c t)"))
 
-        def gate(s, b):
-            ps = first_stage(s, b, 1)
-            g = work.tile([P, D], F32, name="th", bufs=4, align_bytes=64)
+        gps = {}
+
+        def gate_t(s, b):
+            ps = psum.tile([P, D], F32, name="mm", bufs=4)
+            gps[s, b] = ps
+            mx1(ps[:], s, b, 1, slice(0, D))
+
+        def gate_s(s, b):
+            ps = gps[s, b]
+            g = work.tile([P, D], F32, name="th", bufs=8, align_bytes=64)
             th[s][b] = g
             nc.scalar.activation(out=g[:], in_=ps[:], func=ACT.Tanh, scale=0.5)
 
         def rowmax(b, h):
-            junk = work.tile([P, R], BF16, name="junk", bufs=2)
-            nc.vector.tensor_scalar(out=junk[:], in0=z_sb[b][:, h, :], scalar1=-1.0, scalar2=None, op0=ALU.mult, op1=ALU.min, accum_out=negmax[b][:, h : h + 1])
+            junk = work.tile([P, R], BF16, name="junk", bufs=4)
+            nc.vector.tensor_scalar(out=junk[:], in0=z_sb[b // 2][:, h, b % 2, :], scalar1=-1.0, scalar2=None, op0=ALU.mult, op1=ALU.min, accum_out=negmax[b][:, h : h + 1])
 
         def expo(b, h):
-            e = work.tile([P, R], F32, name="e", bufs=8, align_bytes=64)
+            e = work.tile([P, R], F32, name="e", bufs=16, align_bytes=64)
             e_sb[b][h] = e
-            nc.scalar.activation(out=e[:], in_=z_sb[b][:, h, :], func=ACT.Exp, bias=negmax[b][:, h : h + 1], scale=1.0, accum_out=sums[b][:, h : h + 1])
+            nc.scalar.activation(out=e[:], in_=z_sb[b // 2][:, h, b % 2, :], func=ACT.Exp, bias=negmax[b][:, h : h + 1], scale=1.0, accum_out=sums[b][:, h : h + 1])
 
-        def weights(b):
+        def inv(b):
             nc.vector.reciprocal(out=rinv[b][:], in_=sums[b][:])
-            a = work.tile([P, H, R], BF16, name="a_bf", bufs=2, align_bytes=64)
-            a_bf[b] = a
-            for h in range(H):
-                nc.vector.scalar_tensor_tensor(out=a[:, h, :], in0=e_sb[b][h][:], scalar=rinv[b][:, h : h + 1], in1=c_half[:, h, :], op0=ALU.mult, op1=ALU.mult)
 
-        def turn_weights(b):
-            ai = work.tile([P, H * P, 4], BF16, name="ain", bufs=2, align_bytes=64)
-            ain[b] = ai
-            for hh in range(2):
-                tr = psum.tile([P, 2, 2, P], F32, name="tr", bufs=4)
-                for k in range(2):
-                    aw = a_bf[b][:, 2 * hh + k, :].bitcast(F32)
-                    for u in range(2):
-                        nc.tensor.transpose(tr[:, k, u, :], aw[:, u::2], ident[:])
-                dst = ai[:, 2 * hh * P : 2 * (hh + 1) * P, :].rearrange("p c t -> p (c t)").bitcast(F32).rearrange("p (k q u) -> p k q u", k=2, u=2)
-                nc.scalar.copy(out=dst, in_=tr[:].rearrange("p k u q -> p k q u"))
+        def wgt(b, h):
+            nc.vector.scalar_tensor_tensor(out=a_bf[b][:, h, :], in0=e_sb[b][h][:], scalar=rinv[b][:, h : h + 1], in1=c_all[:, h, :], op0=ALU.mult, op1=ALU.mult)
+
+        aps = {}
+
+        def turn_a(b, hh):
+            tr = psum.tile([P, 2, 2, P], F32, name="tr", bufs=4)
+            for k in range(2):
+                aw = a_bf[b][:, 2 * hh + k, :].bitcast(F32)
+                for u in range(2):
+                    nc.tensor.transpose(tr[:, k, u, :], aw[:, u::2], ident[:])
+            aps[b, hh] = tr
+
+        def aevac(b, hh, eng="S"):
+            tr = aps[b, hh]
+            dst = ain[b][:, 2 * hh * P : 2 * (hh + 1) * P, :].rearrange("p c t -> p (c t)").bitcast(F32).rearrange("p (k q u) -> p k q u", k=2, u=2)
+            src = tr[:].rearrange("p k u q -> p k q u")
+            if eng == "S":
+                nc.scalar.copy(out=dst, in_=src)
+            else:
+                nc.vector.tensor_copy(out=dst, in_=src)
 
         def qa(b):
             nc.vector.quantize_mx(out=aq[b][:].bitcast(E4M3X4), scales=asc[b][:], in_=ain[b][:].rearrange("p c t -> p (c t)"))
 
-        def product(s, b):
+        ps_of = {}
+
+        def umm(s, b):
             ps = psum.tile([P, D], F32, name="mm", bufs=4)
+            ps_of[s, b] = ps
             for h in range(H):
                 cols = slice(h * P, (h + 1) * P)
                 nc.tensor.matmul_mx(out=ps[:, cols], lhsT=aq[b][:, cols].bitcast(E4M3X4), lhsT_scale=asc[b][:, cols],
                                     rhs=vq[s][:, cols].bitcast(E4M3X4), rhs_scale=vs[s][:, cols], start=True, stop=True)
-            o = work.tile([P, D], F32, name="o", bufs=4, align_bytes=64)
-            nc.vector.scalar_tensor_tensor(out=o[:], in0=th[s][b][:], scalar=1.0, in1=ps[:], op0=ALU.add, op1=ALU.mult)
-            nc.sync.dma_start(out=out_0[s].rearrange("(p b) d -> b p d", b=4)[b], in_=o[:])
-            if b % 2 == 0:
-                obt = work.tile([P, 2, D], BF16, name="ob", bufs=4, align_bytes=64)
-                ob[s][b // 2] = obt
-            nc.scalar.copy(out=ob[s][b // 2][:, b % 2, :], in_=o[:])
 
-        def turn_out(s, w):
-            tr = psum.tile([P, 2, 2, P], F32, name="tr", bufs=4)
-            for k in range(2):
-                ow = ob[s][w][:, k, :].bitcast(F32)
-                for u in range(2):
-                    nc.tensor.transpose(tr[:, k, u, :], ow[:, u::2], ident[:])
-            dst = oin[s][:].rearrange("p c t -> p (c t)").bitcast(F32).rearrange("p (q x) -> p q x", x=8)
-            nc.scalar.copy(out=dst[:, :, 4 * w : 4 * w + 4], in_=tr[:].rearrange("p k u q -> p q (k u)"))
+        def prod(s, b):
+            o = work.tile([P, D], F32, name="o", bufs=8, align_bytes=64)
+            o_sb[s][b] = o
+            nc.vector.scalar_tensor_tensor(out=o[:], in0=th[s][b][:], scalar=1.0, in1=ps_of[s, b][:], op0=ALU.add, op1=ALU.mult)
+            nc.sync.dma_start(out=out_0[s].rearrange("(p b) d -> b p d", b=4)[b], in_=o[:])
+
+        def cast(s, b, eng="S"):
+            dst, src = ob[s][b // 2][:, b % 2, :], o_sb[s][b][:]
+            if eng == "S":
+                nc.scalar.copy(out=dst, in_=src)
+            elif eng == "V":
+                nc.vector.tensor_copy(out=dst, in_=src)
+            else:
+                nc.gpsimd.tensor_scalar(out=dst, in0=src, scalar1=1.0, scalar2=0.0, op0=ALU.mult, op1=ALU.add)
+
+        ops = {}
+
+        def turn_o(s, b):
+            w, k = b // 2, b % 2
+            if k == 0:
+                tr = psum.tile([P, 2, 2, P], F32, name="tr", bufs=4)
+                ops[s, w] = tr
+            ow = ob[s][w][:, k, :].bitcast(F32)
+            for u in range(2):
+                nc.tensor.transpose(ops[s, w][:, k, u, :], ow[:, u::2], ident[:])
+
+        def oevac(s, w, eng="S"):
+            tr = ops[s, w]
+            dst = oin[s][:].rearrange("p c t -> p (c t)").bitcast(F32).rearrange("p (q x) -> p q x", x=8)[:, :, 4 * w : 4 * w + 4]
+            src = tr[:].rearrange("p k u q -> p q (k u)")
+            if eng == "S":
+                nc.scalar.copy(out=dst, in_=src)
+            elif eng == "V":
+                nc.vector.tensor_copy(out=dst, in_=src)
 
         def planes(s):
             nc.vector.quantize_mx(out=oq[s][:].bitcast(E4M3X4), scales=osc[s][:], in_=oin[s][:].rearrange("p c t -> p (c t)"))
             cols = slice(s * R, (s + 1) * R)
             nc.sync.dma_start(out=out_1[0, :, cols, :].rearrange("p m t -> p (m t)").bitcast(I32), in_=oq[s][:].bitcast(I32))
             for q in range(4):
-                nc.sync.dma_start(out=out_2[0, 4 * q : 4 * q + 4, cols].bitcast(I32), in_=osc[s][32 * q : 32 * q + 4, :].bitcast(I32))
+                (nc.scalar if s == 1 else nc.sync).dma_start(out=out_2[0, 4 * q : 4 * q + 4, cols].bitcast(I32), in_=osc[s][32 * q : 32 * q + 4, :].bitcast(I32))
 
-        def softmax_head(b):
-            for h in range(H):
-                rowmax(b, h)
-                expo(b, h)
-
-        stats(0)
-        softmax_head(0)
-        for j in range(4):
-            norm(0, j)
-            rowmax(1, j)
-            expo(1, j)
+        load_small()
+        load_m(0)
+        load_vectors()
+        load_z(0)
+        load_m(1)
+        load_words()
+        load_scales()
+        load_c()
+        load_z(1)
+        constants()
+        bn(0, 0)
+        bn(0, 1)
+        aggr(0, 0, 2)
+        norm(0, 0)
+        norm(0, 1)
+        sstat_sum(0, 2, 4)
+        rowmax(1, 1)
+        sstat_sq(0, 2, 4)
+        rowmax(0, 1)
+        turn_m(0, 0)
+        rowmax(0, 0)
+        norm(0, 3)
+        norm(0, 2)
+        expo(0, 1)
+        turn_m(0, 1)
+        rowmax(1, 0)
+        sstat_sum(1, 2, 4)
+        rowmax(0, 3)
+        rowmax(1, 3)
+        sstat_sq(1, 2, 4)
+        turn_m(0, 3)
+        bn(1, 1)
+        gainm(0, 0)
+        norm(1, 3)
+        expo(1, 3)
+        norm(1, 2)
+        rowmax(0, 2)
+        turn_m(0, 2)
+        bn(1, 0)
+        expo(0, 0)
+        rowmax(1, 2)
+        aggr(1, 0, 2)
+        gainm(0, 3)
+        gainm(0, 1)
+        turn_m(1, 2)
+        gainm(0, 2)
+        expo(0, 2)
+        expo(1, 1)
+        rowmax(2, 1)
+        rowmax(3, 0)
+        turn_m(1, 3)
+        rowmax(2, 0)
+        rowmax(3, 2)
+        expo(0, 3)
+        expo(1, 0)
+        norm(1, 1)
+        expo(1, 2)
+        norm(1, 0)
+        rowmax(2, 2)
+        expo(2, 0)
         qmn(0)
-        values(0)
-        stats(1)
-        weights(0)
-        turn_weights(0)
-        for j in range(4):
-            norm(1, j)
-        qa(0)
+        gainm(1, 2)
+        rowmax(3, 1)
+        expo(3, 0)
+        gate_t(0, 0)
+        inv(1)
+        vals_t(0, 3)
+        turn_m(1, 1)
+        inv(0)
+        rowmax(3, 3)
+        vals_t(0, 0)
+        rowmax(2, 3)
+        wgt(1, 0)
+        turn_m(1, 0)
+        gate_s(0, 0)
+        wgt(0, 0)
+        wgt(0, 1)
+        gainm(1, 3)
+        expo(2, 2)
+        gainm(1, 1)
+        expo(2, 3)
+        vals_t(0, 2)
+        wgt(1, 1)
+        expo(3, 2)
+        turn_a(0, 0)
+        expo(2, 1)
+        vals_s(0, 0)
+        vals_s(0, 2)
+        vals_s(0, 3)
+        turn_a(1, 0)
+        inv(2)
+        expo(3, 1)
+        gate_t(0, 3)
+        gainm(1, 0)
+        wgt(2, 2)
+        gate_s(0, 3)
+        gate_t(0, 1)
         qmn(1)
-        values(1)
-        softmax_head(2)
+        wgt(2, 1)
+        expo(3, 3)
+        aevac(0, 0, 'S')
+        vals_t(0, 1)
+        vals_t(1, 2)
+        wgt(0, 3)
+        wgt(0, 2)
+        wgt(2, 0)
+        inv(3)
+        gate_s(0, 1)
+        wgt(1, 3)
+        wgt(1, 2)
+        gate_t(0, 2)
+        vals_s(0, 1)
+        turn_a(0, 1)
+        wgt(3, 0)
+        turn_a(2, 0)
+        vals_t(1, 1)
+        vals_t(1, 3)
+        vals_s(1, 2)
+        vint(0, 0)
+        gate_s(0, 2)
+        vint(0, 1)
+        vals_s(1, 1)
+        aevac(1, 0, 'S')
+        wgt(3, 1)
+        gate_t(1, 2)
+        vals_t(1, 0)
+        vals_s(1, 0)
+        vals_s(1, 3)
+        turn_a(1, 1)
+        turn_a(3, 0)
+        aevac(0, 1, 'S')
+        aevac(2, 0, 'S')
+        wgt(3, 3)
+        wgt(3, 2)
+        aevac(1, 1, 'S')
+        gate_t(1, 3)
+        gate_s(1, 2)
+        wgt(2, 3)
+        turn_a(3, 1)
+        qa(0)
+        gate_t(1, 0)
         qv(0)
-        weights(1)
-        turn_weights(1)
-        gate(0, 0)
-        gate(1, 0)
-        qv(1)
+        aevac(3, 0, 'S')
+        gate_t(1, 1)
+        aevac(3, 1, 'S')
+        turn_a(2, 1)
         qa(1)
-        product(0, 0)
-        product(1, 0)
-        softmax_head(3)
-        weights(2)
-        turn_weights(2)
-        gate(0, 1)
-        gate(1, 1)
-        product(0, 1)
-        product(1, 1)
-        turn_out(0, 0)
-        turn_out(1, 0)
-        qa(2)
-        weights(3)
-        turn_weights(3)
-        gate(0, 2)
-        gate(1, 2)
-        product(0, 2)
-        product(1, 2)
+        gate_s(1, 0)
+        vint(1, 1)
+        gate_s(1, 3)
+        vint(1, 0)
         qa(3)
-        gate(0, 3)
-        gate(1, 3)
-        product(0, 3)
-        turn_out(0, 1)
-        product(1, 3)
-        turn_out(1, 1)
-        planes(0)
+        umm(0, 1)
+        qv(1)
+        umm(0, 0)
+        aevac(2, 1, 'S')
+        prod(0, 1)
+        gate_s(1, 1)
+        prod(0, 0)
+        qa(2)
+        umm(1, 0)
+        prod(1, 0)
+        umm(1, 1)
+        cast(0, 0, 'S')
+        prod(1, 1)
+        umm(0, 3)
+        umm(1, 2)
+        cast(0, 1, 'S')
+        prod(1, 2)
+        prod(0, 3)
+        umm(1, 3)
+        cast(1, 0, 'S')
+        prod(1, 3)
+        cast(1, 1, 'S')
+        umm(0, 2)
+        cast(1, 2, 'S')
+        turn_o(1, 0)
+        turn_o(0, 0)
+        prod(0, 2)
+        cast(0, 3, 'S')
+        turn_o(1, 1)
+        cast(1, 3, 'S')
+        oevac(1, 0, 'S')
+        turn_o(1, 2)
+        turn_o(0, 1)
+        cast(0, 2, 'S')
+        turn_o(1, 3)
+        oevac(1, 1, 'S')
         planes(1)
+        turn_o(0, 2)
+        oevac(0, 0, 'S')
+        turn_o(0, 3)
+        oevac(0, 1, 'S')
+        planes(0)

@@ -249,7 +249,8 @@ def tile_msapairweightedaveraging_x2_kernel(tc, m, ln_g, w_v_words, w_v_scales, 
             nc.sync.dma_start(out=out_0[s].rearrange("(p b) d -> b p d", b=4)[b], in_=o[:])
 
         def cast(s, b, eng="S"):
-            dst, src = ob[s][b // 2][:, b % 2, :], o_sb[s][b][:]
+            dst = ob[s][b // 2][:, b % 2, :].rearrange("q (u p e) -> q u p e", u=2, e=2)
+            src = o_sb[s][b][:].rearrange("q (p u e) -> q u p e", u=2, e=2)
             if eng == "S":
                 nc.scalar.copy(out=dst, in_=src)
             elif eng == "V":
@@ -266,7 +267,7 @@ def tile_msapairweightedaveraging_x2_kernel(tc, m, ln_g, w_v_words, w_v_scales, 
                 ops[s, w] = tr
             ow = ob[s][w][:, k, :].bitcast(F32)
             for u in range(2):
-                nc.tensor.transpose(ops[s, w][:, k, u, :], ow[:, u::2], ident[:])
+                nc.tensor.transpose(ops[s, w][:, k, u, :], ow[:, u * P : (u + 1) * P], ident[:])
 
         def oevac(s, w, eng="S"):
             tr = ops[s, w]
@@ -291,190 +292,190 @@ def tile_msapairweightedaveraging_x2_kernel(tc, m, ln_g, w_v_words, w_v_scales, 
         load_m(1)
         load_words()
         load_scales()
-        load_c()
         load_z(1)
+        load_c()
         constants()
         bn(0, 0)
         bn(0, 1)
         aggr(0, 0, 2)
-        norm(0, 0)
-        norm(0, 1)
+        rowmax(1, 0)
+        rowmax(0, 0)
         sstat_sum(0, 2, 4)
+        norm(0, 1)
         rowmax(1, 1)
         sstat_sq(0, 2, 4)
-        rowmax(0, 1)
-        turn_m(0, 0)
-        rowmax(0, 0)
-        norm(0, 3)
-        norm(0, 2)
-        expo(0, 1)
         turn_m(0, 1)
-        rowmax(1, 0)
-        sstat_sum(1, 2, 4)
+        rowmax(0, 1)
+        expo(1, 1)
+        rowmax(1, 2)
+        norm(0, 0)
+        turn_m(0, 0)
         rowmax(0, 3)
         rowmax(1, 3)
-        sstat_sq(1, 2, 4)
-        turn_m(0, 3)
+        norm(0, 3)
         bn(1, 1)
-        gainm(0, 0)
-        norm(1, 3)
-        expo(1, 3)
-        norm(1, 2)
-        rowmax(0, 2)
-        turn_m(0, 2)
         bn(1, 0)
-        expo(0, 0)
-        rowmax(1, 2)
+        rowmax(0, 2)
+        norm(0, 2)
         aggr(1, 0, 2)
-        gainm(0, 3)
-        gainm(0, 1)
-        turn_m(1, 2)
-        gainm(0, 2)
-        expo(0, 2)
-        expo(1, 1)
-        rowmax(2, 1)
-        rowmax(3, 0)
-        turn_m(1, 3)
-        rowmax(2, 0)
-        rowmax(3, 2)
-        expo(0, 3)
         expo(1, 0)
-        norm(1, 1)
-        expo(1, 2)
+        turn_m(0, 3)
         norm(1, 0)
-        rowmax(2, 2)
-        expo(2, 0)
-        qmn(0)
-        gainm(1, 2)
-        rowmax(3, 1)
-        expo(3, 0)
-        gate_t(0, 0)
-        inv(1)
-        vals_t(0, 3)
-        turn_m(1, 1)
-        inv(0)
-        rowmax(3, 3)
-        vals_t(0, 0)
-        rowmax(2, 3)
-        wgt(1, 0)
+        turn_m(0, 2)
+        gainm(0, 1)
+        gainm(0, 0)
+        norm(1, 1)
         turn_m(1, 0)
-        gate_s(0, 0)
-        wgt(0, 0)
-        wgt(0, 1)
-        gainm(1, 3)
-        expo(2, 2)
-        gainm(1, 1)
-        expo(2, 3)
+        gainm(0, 3)
+        expo(0, 1)
+        expo(1, 2)
+        gainm(0, 2)
+        rowmax(3, 1)
+        sstat_sum(1, 2, 4)
+        rowmax(2, 1)
+        expo(0, 3)
+        turn_m(1, 1)
+        qmn(0)
+        sstat_sq(1, 2, 4)
+        expo(0, 2)
+        gate_t(0, 0)
+        expo(1, 3)
+        rowmax(2, 0)
         vals_t(0, 2)
-        wgt(1, 1)
-        expo(3, 2)
-        turn_a(0, 0)
-        expo(2, 1)
-        vals_s(0, 0)
+        rowmax(3, 3)
+        gainm(1, 1)
+        expo(0, 0)
+        gate_s(0, 0)
         vals_s(0, 2)
-        vals_s(0, 3)
-        turn_a(1, 0)
-        inv(2)
+        inv(0)
+        vals_t(0, 3)
+        rowmax(2, 3)
+        rowmax(2, 2)
+        vals_t(0, 0)
+        expo(3, 3)
+        rowmax(3, 2)
+        expo(2, 3)
+        vals_t(0, 1)
+        inv(1)
+        gainm(1, 0)
+        expo(2, 0)
+        vals_s(0, 1)
         expo(3, 1)
         gate_t(0, 3)
-        gainm(1, 0)
-        wgt(2, 2)
+        wgt(1, 2)
+        norm(1, 2)
+        expo(2, 2)
+        wgt(0, 0)
+        wgt(1, 1)
+        turn_m(1, 2)
+        expo(3, 2)
+        norm(1, 3)
         gate_s(0, 3)
-        gate_t(0, 1)
+        wgt(0, 1)
+        wgt(1, 0)
+        gainm(1, 2)
+        turn_m(1, 3)
+        gainm(1, 3)
+        turn_a(0, 0)
+        wgt(1, 3)
+        vals_s(0, 3)
         qmn(1)
-        wgt(2, 1)
-        expo(3, 3)
-        aevac(0, 0, 'S')
-        vals_t(0, 1)
+        rowmax(3, 0)
+        turn_a(1, 0)
+        expo(2, 1)
+        vals_s(0, 0)
+        inv(2)
+        turn_a(1, 1)
+        expo(3, 0)
         vals_t(1, 2)
-        wgt(0, 3)
         wgt(0, 2)
+        gate_t(1, 3)
+        aevac(0, 0, 'S')
+        vals_s(1, 2)
+        gate_t(1, 2)
+        gate_t(0, 1)
+        gate_s(1, 3)
+        vint(0, 0)
+        vals_t(1, 3)
         wgt(2, 0)
         inv(3)
-        gate_s(0, 1)
-        wgt(1, 3)
-        wgt(1, 2)
-        gate_t(0, 2)
-        vals_s(0, 1)
-        turn_a(0, 1)
-        wgt(3, 0)
-        turn_a(2, 0)
-        vals_t(1, 1)
-        vals_t(1, 3)
-        vals_s(1, 2)
-        vint(0, 0)
-        gate_s(0, 2)
-        vint(0, 1)
-        vals_s(1, 1)
-        aevac(1, 0, 'S')
-        wgt(3, 1)
-        gate_t(1, 2)
-        vals_t(1, 0)
-        vals_s(1, 0)
-        vals_s(1, 3)
-        turn_a(1, 1)
-        turn_a(3, 0)
-        aevac(0, 1, 'S')
-        aevac(2, 0, 'S')
-        wgt(3, 3)
-        wgt(3, 2)
-        aevac(1, 1, 'S')
-        gate_t(1, 3)
         gate_s(1, 2)
+        wgt(2, 2)
+        gate_s(0, 1)
+        vals_t(1, 1)
+        vals_s(1, 3)
+        wgt(2, 1)
+        gate_t(0, 2)
+        wgt(3, 1)
+        wgt(3, 0)
+        vals_t(1, 0)
         wgt(2, 3)
-        turn_a(3, 1)
-        qa(0)
         gate_t(1, 0)
+        turn_a(3, 0)
+        wgt(0, 3)
+        vals_s(1, 0)
+        vals_s(1, 1)
+        turn_a(0, 1)
+        wgt(3, 2)
+        vint(0, 1)
+        aevac(1, 0, 'S')
+        wgt(3, 3)
         qv(0)
-        aevac(3, 0, 'S')
-        gate_t(1, 1)
-        aevac(3, 1, 'S')
-        turn_a(2, 1)
-        qa(1)
-        gate_s(1, 0)
-        vint(1, 1)
-        gate_s(1, 3)
+        aevac(1, 1, 'S')
+        gate_s(0, 2)
+        turn_a(3, 1)
+        aevac(0, 1, 'S')
         vint(1, 0)
-        qa(3)
-        umm(0, 1)
-        qv(1)
-        umm(0, 0)
+        vint(1, 1)
+        turn_a(2, 1)
+        aevac(3, 0, 'S')
+        aevac(3, 1, 'S')
+        gate_s(1, 0)
         aevac(2, 1, 'S')
-        prod(0, 1)
-        gate_s(1, 1)
-        prod(0, 0)
-        qa(2)
+        turn_a(2, 0)
+        gate_t(1, 1)
+        qa(0)
+        qv(1)
         umm(1, 0)
-        prod(1, 0)
-        umm(1, 1)
-        cast(0, 0, 'S')
-        prod(1, 1)
-        umm(0, 3)
-        umm(1, 2)
-        cast(0, 1, 'S')
-        prod(1, 2)
-        prod(0, 3)
+        qa(3)
+        aevac(2, 0, 'S')
+        qa(1)
         umm(1, 3)
-        cast(1, 0, 'S')
+        qa(2)
+        prod(1, 0)
+        umm(1, 2)
         prod(1, 3)
-        cast(1, 1, 'S')
+        gate_s(1, 1)
+        prod(1, 2)
+        umm(1, 1)
+        cast(1, 0, 'S')
         umm(0, 2)
+        umm(0, 1)
+        prod(1, 1)
         cast(1, 2, 'S')
-        turn_o(1, 0)
-        turn_o(0, 0)
+        cast(1, 1, 'S')
         prod(0, 2)
-        cast(0, 3, 'S')
-        turn_o(1, 1)
-        cast(1, 3, 'S')
-        oevac(1, 0, 'S')
-        turn_o(1, 2)
-        turn_o(0, 1)
+        cast(1, 3, 'V')
+        prod(0, 1)
+        umm(0, 0)
+        umm(0, 3)
         cast(0, 2, 'S')
+        prod(0, 0)
+        turn_o(1, 2)
+        cast(0, 1, 'S')
         turn_o(1, 3)
+        turn_o(1, 0)
+        cast(0, 0, 'S')
         oevac(1, 1, 'S')
-        planes(1)
+        prod(0, 3)
+        turn_o(1, 1)
+        cast(0, 3, 'V')
         turn_o(0, 2)
-        oevac(0, 0, 'S')
         turn_o(0, 3)
+        oevac(1, 0, 'S')
+        planes(1)
+        turn_o(0, 0)
+        turn_o(0, 1)
         oevac(0, 1, 'S')
+        oevac(0, 0, 'S')
         planes(0)

@@ -36,7 +36,9 @@ def tile_msapairweightedaveraging_x2_kernel(tc, m, ln_g, w_v_words, w_v_scales, 
         ident = keep.tile([P, P], F32, name="ident", align_bytes=64)
         half_pow = keep.tile([P, 4], F32, name="half_pow")
         tmask_f = keep.tile([P, S, 4], F32, name="tmask_f")
-        c_all = keep.tile([P, H, R], BF16, name="c_all", align_bytes=64)
+        crow = keep.tile([P, R], BF16, name="crow", align_bytes=64)
+        ident_bf = keep.tile([P, P], BF16, name="ident_bf", align_bytes=64)
+        cps = [psum.tile([P, 2, R], BF16, name=f"cps{i}", bufs=1) for i in range(2)]
 
         def load_m(s):
             src = m[s].rearrange("(p t) d -> p t d", t=4)
@@ -56,6 +58,8 @@ def tile_msapairweightedaveraging_x2_kernel(tc, m, ln_g, w_v_words, w_v_scales, 
         def load_small():
             for i in range(2):
                 nc.vector.memset(wsc[i][:].bitcast(I32), 0)
+            nc.vector.memset(crow[:], 0.0)
+            nc.scalar.dma_start(out=crow[0:H, :], in_=c)
             warm = keep.tile([P, 1], F32, name="warm")
             nc.vector.memset(warm[:], 0.0)
             nc.scalar.activation(out=warm[:], in_=warm[:], func=ACT.Exp)
@@ -74,8 +78,10 @@ def tile_msapairweightedaveraging_x2_kernel(tc, m, ln_g, w_v_words, w_v_scales, 
             nc.gpsimd.memset(half_pow[:], -0.5)
             nc.gpsimd.tensor_scalar(out=tmask_f[:], in0=tmask[:], scalar1=0.5, scalar2=0.0, op0=ALU.mult, op1=ALU.add)
 
-        def load_c():
-            nc.sync.dma_start(out=c_all[:].rearrange("p h j -> p (h j)"), in_=c.rearrange("h j -> (h j)").partition_broadcast(P))
+        def spread_c():
+            nc.vector.tensor_copy(out=ident_bf[:], in_=ident[:])
+            for h in range(H):
+                nc.tensor.matmul(out=cps[h // 2][:, h % 2, :], lhsT=ident_bf[:, h : h + 1].to_broadcast([P, P]), rhs=crow[:], start=True, stop=True)
 
         st = [keep.tile([P, 4, 6], F32, name=f"st{s}") for s in range(S)]
         mv = [keep.tile([P, 4, 2], F32, name=f"mv{s}") for s in range(S)]
@@ -146,7 +152,7 @@ def tile_msapairweightedaveraging_x2_kernel(tc, m, ln_g, w_v_words, w_v_scales, 
         tr_of = {}
 
         def turn_m(s, j):
-            tr = psum.tile([P, 4, P], F32, name="tr", bufs=4)
+            tr = psum.tile([P, 4, P], F32, name="tr", bufs=3)
             tr_of[s, j] = tr
             for u in range(4):
                 nc.tensor.transpose(tr[:, u, :], xn_of[s, j][:, u, :], ident[:])
@@ -166,7 +172,7 @@ def tile_msapairweightedaveraging_x2_kernel(tc, m, ln_g, w_v_words, w_v_scales, 
         vps = {}
 
         def vals_t(s, j):
-            ps = psum.tile([P, D], F32, name="mm", bufs=4)
+            ps = psum.tile([P, D], F32, name="mm", bufs=3)
             vps[s, j] = ps
             mx1(ps[:], s, j, 0, slice(0, D))
 
@@ -177,7 +183,7 @@ def tile_msapairweightedaveraging_x2_kernel(tc, m, ln_g, w_v_words, w_v_scales, 
         def vint(s, k):
             fs = slice(k * 256, (k + 1) * 256)
             dst, src = vin[s][:, fs, :], vtmp[s][:, :, fs].rearrange("p t f -> p f t")
-            nc.vector.tensor_copy(out=dst, in_=src)
+            nc.gpsimd.tensor_scalar(out=dst, in0=src, scalar1=1.0, scalar2=0.0, op0=ALU.mult, op1=ALU.add)
 
         def qv(s):
             nc.vector.quantize_mx(out=vq[s][:].bitcast(E4M3X4), scales=vs[s][:], in_=vin[s][:].rearrange("p c t -> p (c t)"))
@@ -185,7 +191,7 @@ def tile_msapairweightedaveraging_x2_kernel(tc, m, ln_g, w_v_words, w_v_scales, 
         gps = {}
 
         def gate_t(s, b):
-            ps = psum.tile([P, D], F32, name="mm", bufs=4)
+            ps = psum.tile([P, D], F32, name="mm", bufs=3)
             gps[s, b] = ps
             mx1(ps[:], s, b, 1, slice(0, D))
 
@@ -208,12 +214,12 @@ def tile_msapairweightedaveraging_x2_kernel(tc, m, ln_g, w_v_words, w_v_scales, 
             nc.vector.reciprocal(out=rinv[b][:], in_=sums[b][:])
 
         def wgt(b, h):
-            nc.vector.scalar_tensor_tensor(out=a_bf[b][:, h, :], in0=e_sb[b][h][:], scalar=rinv[b][:, h : h + 1], in1=c_all[:, h, :], op0=ALU.mult, op1=ALU.mult)
+            nc.vector.scalar_tensor_tensor(out=a_bf[b][:, h, :], in0=e_sb[b][h][:], scalar=rinv[b][:, h : h + 1], in1=cps[h // 2][:, h % 2, :], op0=ALU.mult, op1=ALU.mult)
 
         aps = {}
 
         def turn_a(b, hh):
-            tr = psum.tile([P, 2, 2, P], F32, name="tr", bufs=4)
+            tr = psum.tile([P, 2, 2, P], F32, name="tr", bufs=3)
             for k in range(2):
                 aw = a_bf[b][:, 2 * hh + k, :].bitcast(F32)
                 for u in range(2):
@@ -235,7 +241,7 @@ def tile_msapairweightedaveraging_x2_kernel(tc, m, ln_g, w_v_words, w_v_scales, 
         ps_of = {}
 
         def umm(s, b):
-            ps = psum.tile([P, D], F32, name="mm", bufs=4)
+            ps = psum.tile([P, D], F32, name="mm", bufs=3)
             ps_of[s, b] = ps
             for h in range(H):
                 cols = slice(h * P, (h + 1) * P)
@@ -263,7 +269,7 @@ def tile_msapairweightedaveraging_x2_kernel(tc, m, ln_g, w_v_words, w_v_scales, 
         def turn_o(s, b):
             w, k = b // 2, b % 2
             if k == 0:
-                tr = psum.tile([P, 2, 2, P], F32, name="tr", bufs=4)
+                tr = psum.tile([P, 2, 2, P], F32, name="tr", bufs=3)
                 ops[s, w] = tr
             ow = ob[s][w][:, k, :].bitcast(F32)
             for u in range(2):
@@ -293,189 +299,190 @@ def tile_msapairweightedaveraging_x2_kernel(tc, m, ln_g, w_v_words, w_v_scales, 
         load_words()
         load_scales()
         load_z(1)
-        load_c()
         constants()
+        spread_c()
         bn(0, 0)
         bn(0, 1)
         aggr(0, 0, 2)
-        rowmax(1, 0)
+        norm(0, 1)
         rowmax(0, 0)
         sstat_sum(0, 2, 4)
-        norm(0, 1)
         rowmax(1, 1)
-        sstat_sq(0, 2, 4)
-        turn_m(0, 1)
+        rowmax(1, 0)
         rowmax(0, 1)
-        expo(1, 1)
-        rowmax(1, 2)
+        sstat_sq(0, 2, 4)
+        rowmax(0, 2)
         norm(0, 0)
-        turn_m(0, 0)
-        rowmax(0, 3)
         rowmax(1, 3)
+        rowmax(0, 3)
         norm(0, 3)
         bn(1, 1)
-        bn(1, 0)
-        rowmax(0, 2)
-        norm(0, 2)
-        aggr(1, 0, 2)
-        expo(1, 0)
-        turn_m(0, 3)
-        norm(1, 0)
-        turn_m(0, 2)
-        gainm(0, 1)
-        gainm(0, 0)
-        norm(1, 1)
-        turn_m(1, 0)
-        gainm(0, 3)
-        expo(0, 1)
-        expo(1, 2)
-        gainm(0, 2)
-        rowmax(3, 1)
-        sstat_sum(1, 2, 4)
-        rowmax(2, 1)
-        expo(0, 3)
-        turn_m(1, 1)
-        qmn(0)
-        sstat_sq(1, 2, 4)
-        expo(0, 2)
-        gate_t(0, 0)
-        expo(1, 3)
-        rowmax(2, 0)
-        vals_t(0, 2)
-        rowmax(3, 3)
-        gainm(1, 1)
+        turn_m(0, 1)
         expo(0, 0)
-        gate_s(0, 0)
-        vals_s(0, 2)
+        gainm(0, 1)
+        expo(0, 2)
+        turn_m(0, 0)
+        expo(1, 3)
+        bn(1, 0)
+        sstat_sum(1, 3, 4)
+        norm(0, 2)
+        expo(1, 1)
+        turn_m(0, 3)
+        turn_m(0, 2)
+        bn(1, 2)
+        gainm(0, 0)
+        rowmax(3, 0)
+        sstat_sq(1, 3, 4)
+        expo(0, 3)
+        norm(1, 3)
+        expo(1, 0)
+        aggr(1, 0, 3)
+        turn_m(1, 3)
+        rowmax(3, 1)
+        gainm(0, 3)
+        gainm(0, 2)
+        expo(0, 1)
         inv(0)
+        rowmax(3, 3)
+        qmn(0)
+        expo(3, 0)
+        vals_t(0, 1)
+        rowmax(3, 2)
+        vals_t(0, 0)
+        gainm(1, 3)
+        rowmax(1, 2)
+        expo(3, 1)
         vals_t(0, 3)
         rowmax(2, 3)
-        rowmax(2, 2)
-        vals_t(0, 0)
+        norm(1, 1)
         expo(3, 3)
-        rowmax(3, 2)
-        expo(2, 3)
-        vals_t(0, 1)
-        inv(1)
-        gainm(1, 0)
-        expo(2, 0)
-        vals_s(0, 1)
-        expo(3, 1)
-        gate_t(0, 3)
-        wgt(1, 2)
-        norm(1, 2)
-        expo(2, 2)
-        wgt(0, 0)
-        wgt(1, 1)
-        turn_m(1, 2)
+        norm(1, 0)
         expo(3, 2)
-        norm(1, 3)
-        gate_s(0, 3)
-        wgt(0, 1)
-        wgt(1, 0)
-        gainm(1, 2)
-        turn_m(1, 3)
-        gainm(1, 3)
-        turn_a(0, 0)
-        wgt(1, 3)
-        vals_s(0, 3)
-        qmn(1)
-        rowmax(3, 0)
-        turn_a(1, 0)
-        expo(2, 1)
-        vals_s(0, 0)
-        inv(2)
-        turn_a(1, 1)
-        expo(3, 0)
-        vals_t(1, 2)
-        wgt(0, 2)
-        gate_t(1, 3)
-        aevac(0, 0, 'S')
-        vals_s(1, 2)
-        gate_t(1, 2)
+        vals_s(0, 1)
         gate_t(0, 1)
-        gate_s(1, 3)
-        vint(0, 0)
-        vals_t(1, 3)
-        wgt(2, 0)
+        vals_s(0, 0)
+        expo(1, 2)
         inv(3)
-        gate_s(1, 2)
-        wgt(2, 2)
+        vals_t(0, 2)
+        turn_m(1, 1)
         gate_s(0, 1)
-        vals_t(1, 1)
-        vals_s(1, 3)
-        wgt(2, 1)
-        gate_t(0, 2)
-        wgt(3, 1)
-        wgt(3, 0)
-        vals_t(1, 0)
-        wgt(2, 3)
-        gate_t(1, 0)
-        turn_a(3, 0)
+        rowmax(2, 0)
+        wgt(0, 2)
+        norm(1, 2)
+        turn_m(1, 2)
+        turn_m(1, 0)
+        vals_s(0, 3)
+        rowmax(2, 2)
+        gate_t(0, 0)
+        vals_s(0, 2)
+        expo(2, 3)
+        gate_t(0, 3)
+        expo(2, 2)
+        inv(1)
         wgt(0, 3)
-        vals_s(1, 0)
-        vals_s(1, 1)
+        expo(2, 0)
+        wgt(0, 1)
+        gate_s(0, 3)
+        wgt(0, 0)
+        gainm(1, 1)
+        gainm(1, 2)
+        gate_t(0, 2)
         turn_a(0, 1)
-        wgt(3, 2)
-        vint(0, 1)
-        aevac(1, 0, 'S')
-        wgt(3, 3)
-        qv(0)
-        aevac(1, 1, 'S')
+        turn_a(0, 0)
+        gainm(1, 0)
+        wgt(1, 0)
+        gate_s(0, 0)
+        qmn(1)
+        rowmax(2, 1)
+        wgt(1, 1)
         gate_s(0, 2)
-        turn_a(3, 1)
+        vint(0, 0)
+        vals_t(1, 1)
+        vint(0, 1)
+        vals_t(1, 3)
         aevac(0, 1, 'S')
-        vint(1, 0)
-        vint(1, 1)
-        turn_a(2, 1)
-        aevac(3, 0, 'S')
-        aevac(3, 1, 'S')
-        gate_s(1, 0)
-        aevac(2, 1, 'S')
-        turn_a(2, 0)
+        vals_s(1, 1)
+        wgt(1, 2)
+        wgt(3, 3)
+        vals_t(1, 0)
+        wgt(1, 3)
+        turn_a(1, 0)
+        vals_t(1, 2)
+        vals_s(1, 3)
+        qv(0)
         gate_t(1, 1)
+        aevac(0, 0, 'S')
+        vals_s(1, 0)
+        vals_s(1, 2)
+        expo(2, 1)
+        aevac(1, 0, 'S')
+        wgt(3, 2)
         qa(0)
-        qv(1)
-        umm(1, 0)
-        qa(3)
-        aevac(2, 0, 'S')
+        vint(1, 1)
+        gate_t(1, 2)
+        wgt(3, 1)
+        turn_a(1, 1)
+        inv(2)
+        turn_a(3, 1)
+        aevac(1, 1, 'S')
+        wgt(3, 0)
+        wgt(2, 0)
+        wgt(2, 1)
+        turn_a(3, 0)
+        turn_a(2, 0)
         qa(1)
-        umm(1, 3)
-        qa(2)
-        prod(1, 0)
-        umm(1, 2)
-        prod(1, 3)
+        aevac(3, 1, 'S')
+        umm(0, 0)
+        wgt(2, 3)
+        wgt(2, 2)
+        vint(1, 0)
+        gate_s(1, 2)
         gate_s(1, 1)
-        prod(1, 2)
-        umm(1, 1)
-        cast(1, 0, 'S')
-        umm(0, 2)
+        prod(0, 0)
+        gate_t(1, 0)
         umm(0, 1)
+        aevac(2, 0, 'S')
+        aevac(3, 0, 'S')
+        prod(0, 1)
+        gate_s(1, 0)
+        turn_a(2, 1)
+        qv(1)
+        gate_t(1, 3)
+        qa(3)
+        cast(0, 0, 'S')
+        aevac(2, 1, 'S')
+        qa(2)
+        umm(1, 1)
         prod(1, 1)
-        cast(1, 2, 'S')
+        gate_s(1, 3)
+        umm(1, 0)
+        cast(0, 1, 'S')
+        prod(1, 0)
+        umm(0, 2)
+        umm(0, 3)
+        umm(1, 2)
         cast(1, 1, 'S')
         prod(0, 2)
-        cast(1, 3, 'V')
-        prod(0, 1)
-        umm(0, 0)
-        umm(0, 3)
-        cast(0, 2, 'S')
-        prod(0, 0)
-        turn_o(1, 2)
-        cast(0, 1, 'S')
-        turn_o(1, 3)
-        turn_o(1, 0)
-        cast(0, 0, 'S')
-        oevac(1, 1, 'S')
         prod(0, 3)
-        turn_o(1, 1)
-        cast(0, 3, 'V')
-        turn_o(0, 2)
-        turn_o(0, 3)
-        oevac(1, 0, 'S')
-        planes(1)
         turn_o(0, 0)
+        cast(1, 0, 'S')
+        prod(1, 2)
         turn_o(0, 1)
-        oevac(0, 1, 'S')
+        cast(0, 3, 'V')
+        umm(1, 3)
+        cast(0, 2, 'S')
         oevac(0, 0, 'S')
+        turn_o(0, 2)
+        prod(1, 3)
+        turn_o(0, 3)
+        cast(1, 2, 'S')
+        oevac(0, 1, 'S')
+        cast(1, 3, 'V')
+        turn_o(1, 0)
+        turn_o(1, 1)
+        turn_o(1, 2)
+        oevac(1, 0, 'S')
+        turn_o(1, 3)
         planes(0)
+        oevac(1, 1, 'S')
+        planes(1)

from contextlib import ExitStack

import concourse.mybir as mybir
from concourse.masks import make_identity

S, R, H, E = 2, 512, 4, 128
D = H * E
P = 128
EPS = 1e-5
FLOPS = 2 * (2 * S * R * D * D) + 2 * H * R * R * S * E

F32 = mybir.dt.float32
BF16 = mybir.dt.bfloat16
U32 = mybir.dt.uint32
I32 = mybir.dt.int32
U8 = mybir.dt.uint8
E4M3X4 = mybir.dt.float8_e4m3fn_x4
E2M1X4 = mybir.dt.float4_e2m1fn_x4
ACT = mybir.ActivationFunctionType
ALU = mybir.AluOpType


def tile_msapairweightedaveraging_x2_kernel(tc, m, ln_g, w_v_words, w_v_scales, w_g_words, w_g_scales, t, z, c, out_0, out_1, out_2):
    nc = tc.nc
    with ExitStack() as ctx:
        keep = ctx.enter_context(tc.tile_pool(name="keep", bufs=1))
        work = ctx.enter_context(tc.tile_pool(name="work", bufs=2))
        psum = ctx.enter_context(tc.psum_pool(name="psum", bufs=4))
        ctx.enter_context(tc.manual_schedule())
        m_sb = [keep.tile([P, 4, D], BF16, name=f"m{s}", align_bytes=64) for s in range(S)]
        z_sb = [keep.tile([P, H, 2, R], BF16, name=f"z{w}", align_bytes=64) for w in range(2)]
        gain = keep.tile([P, 4], BF16, name="gain")
        tmask = keep.tile([P, S, 4], BF16, name="tmask")
        words = [keep.tile([P, 2 * D], U8, name=f"words{i}", align_bytes=64) for i in range(2)]
        wsc = [keep.tile([P, D], U8, name=f"wsc{i}", align_bytes=64) for i in range(2)]
        ident = keep.tile([P, P], F32, name="ident", align_bytes=64)
        half_pow = keep.tile([P, 4], F32, name="half_pow")
        tmask_f = keep.tile([P, S, 4], F32, name="tmask_f")
        crow = keep.tile([P, R], BF16, name="crow", align_bytes=64)
        ident_bf = keep.tile([P, P], BF16, name="ident_bf", align_bytes=64)
        cps = [psum.tile([P, 2, R], BF16, name=f"cps{i}", bufs=1) for i in range(2)]

        def load_m(s):
            src = m[s].rearrange("(p t) d -> p t d", t=4)
            for half in range(2):
                nc.sync.dma_start(out=m_sb[s][:, 2 * half : 2 * half + 2, :], in_=src[:, 2 * half : 2 * half + 2, :])

        def load_z(w):
            src = z.rearrange("h (p w b) j -> w p h b j", w=2, b=2)
            for half in range(2):
                hs = slice(2 * half, 2 * half + 2)
                nc.sync.dma_start(out=z_sb[w][:, hs, :, :], in_=src[w][:, hs, :, :])

        def load_words():
            for i, w in enumerate((w_v_words, w_g_words)):
                nc.sync.dma_start(out=words[i][:].bitcast(I32), in_=w[0].bitcast(I32))

        def load_small():
            for i in range(2):
                nc.vector.memset(wsc[i][:].bitcast(I32), 0)
            nc.vector.memset(crow[:], 0.0)
            nc.scalar.dma_start(out=crow[0:H, :], in_=c)
            warm = keep.tile([P, 1], F32, name="warm")
            nc.vector.memset(warm[:], 0.0)
            nc.scalar.activation(out=warm[:], in_=warm[:], func=ACT.Exp)

        def load_vectors():
            nc.sync.dma_start(out=gain[:], in_=ln_g.rearrange("(p t) -> p t", t=4))
            nc.sync.dma_start(out=tmask[:], in_=t.rearrange("s (p t) -> p s t", t=4))

        def load_scales():
            for i, ws in enumerate((w_v_scales, w_g_scales)):
                for q in range(4):
                    nc.sync.dma_start(out=wsc[i][32 * q : 32 * q + 4, :].bitcast(I32), in_=ws[0, 4 * q : 4 * q + 4, :].bitcast(I32))

        def constants():
            make_identity(nc, ident[:])
            nc.gpsimd.memset(half_pow[:], -0.5)
            nc.gpsimd.tensor_scalar(out=tmask_f[:], in0=tmask[:], scalar1=0.5, scalar2=0.0, op0=ALU.mult, op1=ALU.add)

        def spread_c():
            nc.vector.tensor_copy(out=ident_bf[:], in_=ident[:])
            for h in range(H):
                nc.tensor.matmul(out=cps[h // 2][:, h % 2, :], lhsT=ident_bf[:, h : h + 1].to_broadcast([P, P]), rhs=crow[:], start=True, stop=True)

        st = [keep.tile([P, 4, 6], F32, name=f"st{s}") for s in range(S)]
        mv = [keep.tile([P, 4, 2], F32, name=f"mv{s}") for s in range(S)]
        ssum = [keep.tile([P, 4], F32, name=f"ssum{s}") for s in range(S)]
        smean = [keep.tile([P, 4], F32, name=f"smean{s}") for s in range(S)]
        ssq = [keep.tile([P, 4], F32, name=f"ssq{s}") for s in range(S)]
        ve = [keep.tile([P, 4], F32, name=f"ve{s}") for s in range(S)]
        rstd = [keep.tile([P, 4], F32, name=f"rstd{s}") for s in range(S)]
        negmean = [keep.tile([P, 4], F32, name=f"negmean{s}") for s in range(S)]
        nmr = [keep.tile([P, 4], F32, name=f"nmr{s}") for s in range(S)]
        mnb = [keep.tile([P, R, 4], BF16, name=f"mnb{s}", align_bytes=64) for s in range(S)]
        mnq = [keep.tile([P, R], U32, name=f"mnq{s}", align_bytes=64) for s in range(S)]
        mns = [keep.tile([P, R], U8, name=f"mns{s}", align_bytes=64) for s in range(S)]
        vtmp = [keep.tile([P, 4, D], BF16, name=f"vtmp{s}", align_bytes=64) for s in range(S)]
        vin = [keep.tile([P, D, 4], BF16, name=f"vin{s}", align_bytes=64) for s in range(S)]
        vq = [keep.tile([P, D], U32, name=f"vq{s}", align_bytes=64) for s in range(S)]
        vs = [keep.tile([P, D], U8, name=f"vs{s}", align_bytes=64) for s in range(S)]
        negmax = [keep.tile([P, H], F32, name=f"negmax{b}") for b in range(4)]
        sums = [keep.tile([P, H], F32, name=f"sums{b}") for b in range(4)]
        rinv = [keep.tile([P, H], F32, name=f"rinv{b}") for b in range(4)]
        e_sb = [[None] * H for b in range(4)]
        a_bf = [keep.tile([P, H, R], BF16, name=f"a_bf{b}", align_bytes=64) for b in range(4)]
        ain = [keep.tile([P, H * P, 4], BF16, name=f"ain{b}", align_bytes=64) for b in range(4)]
        aq = [keep.tile([P, H * P], U32, name=f"aq{b}", align_bytes=64) for b in range(4)]
        asc = [keep.tile([P, H * P], U8, name=f"asc{b}", align_bytes=64) for b in range(4)]
        th = [[None] * 4 for s in range(S)]
        ob = [[keep.tile([P, 2, D], BF16, name=f"ob{s}{w}", align_bytes=64) for w in range(2)] for s in range(S)]
        oin = [keep.tile([P, R, 4], BF16, name=f"oin{s}", align_bytes=64) for s in range(S)]
        oq = [keep.tile([P, R], U32, name=f"oq{s}", align_bytes=64) for s in range(S)]
        osc = [keep.tile([P, R], U8, name=f"osc{s}", align_bytes=64) for s in range(S)]
        o_sb = [[None] * 4 for s in range(S)]

        def bn(s, j):
            nc.vector.bn_stats(out=st[s][:, j, :], in_=m_sb[s][:, j, :])

        def aggr(s, lo=0, hi=4):
            for j in range(lo, hi):
                nc.vector.bn_aggr(out=mv[s][:, j, :], in_=st[s][:, j, :])
            r = slice(lo, hi)
            nc.gpsimd.tensor_scalar(out=ve[s][:, r], in0=mv[s][:, r, 1], scalar1=EPS, scalar2=1.0, op0=ALU.add, op1=ALU.mult)
            nc.gpsimd.tensor_tensor(out=rstd[s][:, r], in0=ve[s][:, r], in1=half_pow[:, r], op=ALU.pow)
            nc.gpsimd.tensor_scalar(out=negmean[s][:, r], in0=mv[s][:, r, 0], scalar1=-1.0, scalar2=0.0, op0=ALU.mult, op1=ALU.add)

        def sstat_sum(s, lo, hi):
            for j in range(lo, hi):
                sjunk = work.tile([P, D], BF16, name="sjunk", bufs=2)
                nc.scalar.activation(out=sjunk[:], in_=m_sb[s][:, j, :], func=ACT.Copy, accum_out=ssum[s][:, j : j + 1])
            nc.scalar.mul(out=smean[s][:, lo:hi], in_=ssum[s][:, lo:hi], mul=-1.0 / D)

        def sstat_sq(s, lo, hi):
            for j in range(lo, hi):
                sjunk = work.tile([P, D], BF16, name="sjunk", bufs=2)
                nc.scalar.activation(out=sjunk[:], in_=m_sb[s][:, j, :], func=ACT.Square, bias=smean[s][:, j : j + 1], accum_out=ssq[s][:, j : j + 1])
            r = slice(lo, hi)
            nc.gpsimd.tensor_scalar(out=negmean[s][:, r], in0=smean[s][:, r], scalar1=1.0, scalar2=0.0, op0=ALU.mult, op1=ALU.add)
            nc.gpsimd.tensor_scalar(out=ve[s][:, r], in0=ssq[s][:, r], scalar1=1.0 / D, scalar2=EPS, op0=ALU.mult, op1=ALU.add)
            nc.gpsimd.tensor_tensor(out=rstd[s][:, r], in0=ve[s][:, r], in1=half_pow[:, r], op=ALU.pow)


        xn_of = {}

        def norm(s, j):
            xn = work.tile([P, 4, P], F32, name="xn", bufs=8, align_bytes=64)
            xn_of[s, j] = xn
            src = m_sb[s][:, j, :].rearrange("q (p t) -> q t p", t=4)
            nc.gpsimd.tensor_scalar(out=xn[:], in0=src, scalar1=negmean[s][:, j : j + 1], scalar2=rstd[s][:, j : j + 1], op0=ALU.add, op1=ALU.mult)

        tr_of = {}

        def turn_m(s, j):
            tr = psum.tile([P, 4, P], F32, name="tr", bufs=3)
            tr_of[s, j] = tr
            for u in range(4):
                nc.tensor.transpose(tr[:, u, :], xn_of[s, j][:, u, :], ident[:])

        def gainm(s, j):
            nc.vector.tensor_tensor(out=mnb[s][:, j * P : (j + 1) * P, :], in0=tr_of[s, j][:].rearrange("p t q -> p q t"),
                                    in1=gain[:].unsqueeze(1).to_broadcast([P, P, 4]), op=ALU.mult)

        def qmn(s):
            nc.vector.quantize_mx(out=mnq[s][:].bitcast(E4M3X4), scales=mns[s][:], in_=mnb[s][:].rearrange("p c t -> p (c t)"))

        def mx1(out, s, j, i, cols):
            rows = slice(j * P, (j + 1) * P)
            nc.tensor.matmul_mx(out=out, lhsT=mnq[s][:, rows].bitcast(E4M3X4), lhsT_scale=mns[s][:, rows],
                                rhs=words[i][:, 2 * cols.start : 2 * cols.stop].bitcast(E2M1X4), rhs_scale=wsc[i][:, cols], start=True, stop=True)

        vps = {}

        def vals_t(s, j):
            ps = psum.tile([P, D], F32, name="mm", bufs=3)
            vps[s, j] = ps
            mx1(ps[:], s, j, 0, slice(0, D))

        def vals_s(s, j):
            ps = vps[s, j]
            nc.scalar.activation(out=vtmp[s][:, j, :], in_=ps[:], func=ACT.Copy, scale=tmask_f[:, s, j : j + 1])

        def vint(s, k):
            fs = slice(k * 256, (k + 1) * 256)
            dst, src = vin[s][:, fs, :], vtmp[s][:, :, fs].rearrange("p t f -> p f t")
            nc.gpsimd.tensor_scalar(out=dst, in0=src, scalar1=1.0, scalar2=0.0, op0=ALU.mult, op1=ALU.add)

        def qv(s):
            nc.vector.quantize_mx(out=vq[s][:].bitcast(E4M3X4), scales=vs[s][:], in_=vin[s][:].rearrange("p c t -> p (c t)"))

        gps = {}

        def gate_t(s, b):
            ps = psum.tile([P, D], F32, name="mm", bufs=3)
            gps[s, b] = ps
            mx1(ps[:], s, b, 1, slice(0, D))

        def gate_s(s, b):
            ps = gps[s, b]
            g = work.tile([P, D], F32, name="th", bufs=8, align_bytes=64)
            th[s][b] = g
            nc.scalar.activation(out=g[:], in_=ps[:], func=ACT.Tanh, scale=0.5)

        def rowmax(b, h):
            junk = work.tile([P, R], BF16, name="junk", bufs=4)
            nc.vector.tensor_scalar(out=junk[:], in0=z_sb[b // 2][:, h, b % 2, :], scalar1=-1.0, scalar2=None, op0=ALU.mult, op1=ALU.min, accum_out=negmax[b][:, h : h + 1])

        def expo(b, h):
            e = work.tile([P, R], F32, name="e", bufs=16, align_bytes=64)
            e_sb[b][h] = e
            nc.scalar.activation(out=e[:], in_=z_sb[b // 2][:, h, b % 2, :], func=ACT.Exp, bias=negmax[b][:, h : h + 1], scale=1.0, accum_out=sums[b][:, h : h + 1])

        def inv(b):
            nc.vector.reciprocal(out=rinv[b][:], in_=sums[b][:])

        def wgt(b, h):
            nc.vector.scalar_tensor_tensor(out=a_bf[b][:, h, :], in0=e_sb[b][h][:], scalar=rinv[b][:, h : h + 1], in1=cps[h // 2][:, h % 2, :], op0=ALU.mult, op1=ALU.mult)

        aps = {}

        def turn_a(b, hh):
            tr = psum.tile([P, 2, 2, P], F32, name="tr", bufs=3)
            for k in range(2):
                aw = a_bf[b][:, 2 * hh + k, :].bitcast(F32)
                for u in range(2):
                    nc.tensor.transpose(tr[:, k, u, :], aw[:, u::2], ident[:])
            aps[b, hh] = tr

        def aevac(b, hh, eng="S"):
            tr = aps[b, hh]
            dst = ain[b][:, 2 * hh * P : 2 * (hh + 1) * P, :].rearrange("p c t -> p (c t)").bitcast(F32).rearrange("p (k q u) -> p k q u", k=2, u=2)
            src = tr[:].rearrange("p k u q -> p k q u")
            if eng == "S":
                nc.scalar.copy(out=dst, in_=src)
            else:
                nc.vector.tensor_copy(out=dst, in_=src)

        def qa(b):
            nc.vector.quantize_mx(out=aq[b][:].bitcast(E4M3X4), scales=asc[b][:], in_=ain[b][:].rearrange("p c t -> p (c t)"))

        ps_of = {}

        def umm(s, b):
            ps = psum.tile([P, D], F32, name="mm", bufs=3)
            ps_of[s, b] = ps
            for h in range(H):
                cols = slice(h * P, (h + 1) * P)
                nc.tensor.matmul_mx(out=ps[:, cols], lhsT=aq[b][:, cols].bitcast(E4M3X4), lhsT_scale=asc[b][:, cols],
                                    rhs=vq[s][:, cols].bitcast(E4M3X4), rhs_scale=vs[s][:, cols], start=True, stop=True)

        def prod(s, b):
            o = work.tile([P, D], F32, name="o", bufs=8, align_bytes=64)
            o_sb[s][b] = o
            nc.vector.scalar_tensor_tensor(out=o[:], in0=th[s][b][:], scalar=1.0, in1=ps_of[s, b][:], op0=ALU.add, op1=ALU.mult)
            nc.sync.dma_start(out=out_0[s].rearrange("(p b) d -> b p d", b=4)[b], in_=o[:])

        def cast(s, b, eng="S"):
            dst = ob[s][b // 2][:, b % 2, :].rearrange("q (u p e) -> q u p e", u=2, e=2)
            src = o_sb[s][b][:].rearrange("q (p u e) -> q u p e", u=2, e=2)
            if eng == "S":
                nc.scalar.copy(out=dst, in_=src)
            elif eng == "V":
                nc.vector.tensor_copy(out=dst, in_=src)
            else:
                nc.gpsimd.tensor_scalar(out=dst, in0=src, scalar1=1.0, scalar2=0.0, op0=ALU.mult, op1=ALU.add)

        ops = {}

        def turn_o(s, b):
            w, k = b // 2, b % 2
            if k == 0:
                tr = psum.tile([P, 2, 2, P], F32, name="tr", bufs=3)
                ops[s, w] = tr
            ow = ob[s][w][:, k, :].bitcast(F32)
            for u in range(2):
                nc.tensor.transpose(ops[s, w][:, k, u, :], ow[:, u * P : (u + 1) * P], ident[:])

        def oevac(s, w, eng="S"):
            tr = ops[s, w]
            dst = oin[s][:].rearrange("p c t -> p (c t)").bitcast(F32).rearrange("p (q x) -> p q x", x=8)[:, :, 4 * w : 4 * w + 4]
            src = tr[:].rearrange("p k u q -> p q (k u)")
            if eng == "S":
                nc.scalar.copy(out=dst, in_=src)
            elif eng == "V":
                nc.vector.tensor_copy(out=dst, in_=src)

        def planes(s):
            nc.vector.quantize_mx(out=oq[s][:].bitcast(E4M3X4), scales=osc[s][:], in_=oin[s][:].rearrange("p c t -> p (c t)"))
            cols = slice(s * R, (s + 1) * R)
            nc.sync.dma_start(out=out_1[0, :, cols, :].rearrange("p m t -> p (m t)").bitcast(I32), in_=oq[s][:].bitcast(I32))
            for q in range(4):
                (nc.scalar if s == 1 else nc.sync).dma_start(out=out_2[0, 4 * q : 4 * q + 4, cols].bitcast(I32), in_=osc[s][32 * q : 32 * q + 4, :].bitcast(I32))

        load_small()
        load_m(0)
        load_vectors()
        load_z(0)
        load_m(1)
        load_words()
        load_scales()
        load_z(1)
        constants()
        spread_c()
        bn(0, 0)
        bn(0, 1)
        aggr(0, 0, 2)
        norm(0, 1)
        rowmax(0, 0)
        sstat_sum(0, 2, 4)
        rowmax(1, 1)
        rowmax(1, 0)
        rowmax(0, 1)
        sstat_sq(0, 2, 4)
        rowmax(0, 2)
        norm(0, 0)
        rowmax(1, 3)
        rowmax(0, 3)
        norm(0, 3)
        bn(1, 1)
        turn_m(0, 1)
        expo(0, 0)
        gainm(0, 1)
        expo(0, 2)
        turn_m(0, 0)
        expo(1, 3)
        bn(1, 0)
        sstat_sum(1, 3, 4)
        norm(0, 2)
        expo(1, 1)
        turn_m(0, 3)
        turn_m(0, 2)
        bn(1, 2)
        gainm(0, 0)
        rowmax(3, 0)
        sstat_sq(1, 3, 4)
        expo(0, 3)
        norm(1, 3)
        expo(1, 0)
        aggr(1, 0, 3)
        turn_m(1, 3)
        rowmax(3, 1)
        gainm(0, 3)
        gainm(0, 2)
        expo(0, 1)
        inv(0)
        rowmax(3, 3)
        qmn(0)
        expo(3, 0)
        vals_t(0, 1)
        rowmax(3, 2)
        vals_t(0, 0)
        gainm(1, 3)
        rowmax(1, 2)
        expo(3, 1)
        vals_t(0, 3)
        rowmax(2, 3)
        norm(1, 1)
        expo(3, 3)
        norm(1, 0)
        expo(3, 2)
        vals_s(0, 1)
        gate_t(0, 1)
        vals_s(0, 0)
        expo(1, 2)
        inv(3)
        vals_t(0, 2)
        turn_m(1, 1)
        gate_s(0, 1)
        rowmax(2, 0)
        wgt(0, 2)
        norm(1, 2)
        turn_m(1, 2)
        turn_m(1, 0)
        vals_s(0, 3)
        rowmax(2, 2)
        gate_t(0, 0)
        vals_s(0, 2)
        expo(2, 3)
        gate_t(0, 3)
        expo(2, 2)
        inv(1)
        wgt(0, 3)
        expo(2, 0)
        wgt(0, 1)
        gate_s(0, 3)
        wgt(0, 0)
        gainm(1, 1)
        gainm(1, 2)
        gate_t(0, 2)
        turn_a(0, 1)
        turn_a(0, 0)
        gainm(1, 0)
        wgt(1, 0)
        gate_s(0, 0)
        qmn(1)
        rowmax(2, 1)
        wgt(1, 1)
        gate_s(0, 2)
        vint(0, 0)
        vals_t(1, 1)
        vint(0, 1)
        vals_t(1, 3)
        aevac(0, 1, 'S')
        vals_s(1, 1)
        wgt(1, 2)
        wgt(3, 3)
        vals_t(1, 0)
        wgt(1, 3)
        turn_a(1, 0)
        vals_t(1, 2)
        vals_s(1, 3)
        qv(0)
        gate_t(1, 1)
        aevac(0, 0, 'S')
        vals_s(1, 0)
        vals_s(1, 2)
        expo(2, 1)
        aevac(1, 0, 'S')
        wgt(3, 2)
        qa(0)
        vint(1, 1)
        gate_t(1, 2)
        wgt(3, 1)
        turn_a(1, 1)
        inv(2)
        turn_a(3, 1)
        aevac(1, 1, 'S')
        wgt(3, 0)
        wgt(2, 0)
        wgt(2, 1)
        turn_a(3, 0)
        turn_a(2, 0)
        qa(1)
        aevac(3, 1, 'S')
        umm(0, 0)
        wgt(2, 3)
        wgt(2, 2)
        vint(1, 0)
        gate_s(1, 2)
        gate_s(1, 1)
        prod(0, 0)
        gate_t(1, 0)
        umm(0, 1)
        aevac(2, 0, 'S')
        aevac(3, 0, 'S')
        prod(0, 1)
        gate_s(1, 0)
        turn_a(2, 1)
        qv(1)
        gate_t(1, 3)
        qa(3)
        cast(0, 0, 'S')
        aevac(2, 1, 'S')
        qa(2)
        umm(1, 1)
        prod(1, 1)
        gate_s(1, 3)
        umm(1, 0)
        cast(0, 1, 'S')
        prod(1, 0)
        umm(0, 2)
        umm(0, 3)
        umm(1, 2)
        cast(1, 1, 'S')
        prod(0, 2)
        prod(0, 3)
        turn_o(0, 0)
        cast(1, 0, 'S')
        prod(1, 2)
        turn_o(0, 1)
        cast(0, 3, 'V')
        umm(1, 3)
        cast(0, 2, 'S')
        oevac(0, 0, 'S')
        turn_o(0, 2)
        prod(1, 3)
        turn_o(0, 3)
        cast(1, 2, 'S')
        oevac(0, 1, 'S')
        cast(1, 3, 'V')
        turn_o(1, 0)
        turn_o(1, 1)
        turn_o(1, 2)
        oevac(1, 0, 'S')
        turn_o(1, 3)
        planes(0)
        oevac(1, 1, 'S')
        planes(1)
